import numpy as np
import ml_dtypes


def mxq(x, axis, fmt="e4m3"):
    dtype, down = {"e4m3": (ml_dtypes.float8_e4m3fn, 7), "e5m2": (ml_dtypes.float8_e5m2, 14)}[fmt]
    v = np.moveaxis(np.asarray(x, np.float32).astype(ml_dtypes.bfloat16).astype(np.float64), axis, -1)
    blocks = v.reshape(v.shape[:-1] + (-1, 32))
    amax = np.abs(blocks).max(-1, keepdims=True)
    byte = np.maximum(np.where(amax > 0, np.frexp(amax)[1] - 1 + 127, 0) - down, 1)
    scale = np.exp2(byte - 127.0)
    codes = (blocks / scale).astype(np.float32).astype(dtype).astype(np.float64)
    return np.moveaxis((codes * scale).reshape(v.shape), -1, axis)


WIDE = False


def mx_kscale(k):
    if not WIDE:
        return np.ones(k)
    levels = np.array([10, -10, 5, -5, 0])
    if k % 512:
        return np.exp2(np.random.permutation(np.resize(levels, k // 32))).repeat(32)
    a = np.empty((k // 512, 16))
    for p in range(k // 512):
        a[p, :8] = np.random.permutation(np.resize(levels, 8))
        for g in range(8):
            far = levels[np.abs(levels - a[p, g]) >= 10]
            a[p, g + 8] = far[np.random.randint(len(far))]
    return np.exp2(a.ravel()).repeat(32)


def f64(x):
    return np.asarray(x).astype(np.float64)


def striped(idx):
    return np.tile(idx.reshape(-1, 16).T, (8, 1)).astype(np.uint16)


def unstriped(offs):
    return offs[:16].T.reshape(-1).astype(np.int64)


def pack_weight(w):
    k, n = w.shape
    w = f64(np.asarray(w, np.float32).astype(ml_dtypes.bfloat16)).reshape(k // 32, 32, n)
    amax = np.abs(w).max(1)
    byte = np.clip(np.where(amax > 0, np.frexp(amax)[1] - 1 + 127 - 7, 1), 1, 254)
    scaled = (w * np.exp2(127.0 - byte)[:, None, :]).reshape(k, n).astype(np.float32)
    words = np.ascontiguousarray(scaled.reshape(k // 512, 128, 4, n).transpose(0, 1, 3, 2)).astype(ml_dtypes.float8_e4m3fn).view(np.uint8)
    return words, np.ascontiguousarray(byte.astype(np.uint8).reshape(k // 512, 16, n))


def unpack_weight(words, scales):
    g, p, n, _ = words.shape
    vals = np.ascontiguousarray(words).view(ml_dtypes.float8_e4m3fn).astype(np.float64) * np.repeat(np.exp2(scales.astype(np.float64) - 127.0), 8, axis=1)[..., None]
    return vals.transpose(0, 1, 3, 2).reshape(g * 512, n)


def gelu(v):
    return 0.5 * v * (1.0 + np.tanh(np.sqrt(2.0 / np.pi) * (v + 0.044715 * v**3)))


K, T, S, H, N = 1024, 2048, 1024, 512, 128


def setup_inputs():
    n = np.random.standard_normal
    s = mx_kscale(K)[:, None]
    u = mx_kscale(H)
    packed_w2 = pack_weight(n((H, N)) / np.sqrt(H) / u[:, None])
    return {
        "xT": (n((K, T)) * s).astype(np.float32),
        "w1": (n((K, H)) / np.sqrt(K) / s * u).astype(np.float32),
        "w2_words": packed_w2[0],
        "w2_scales": packed_w2[1],
        "pos": (0.5 * n((H, S)) * u[:, None]).astype(np.float32),
        "offs": striped(np.random.permutation(T)[(T * np.random.uniform(0, 1, S) ** 4).astype(np.int64)]),
    }


def reference(xT, w1, w2_words, w2_scales, pos, offs):
    xq = mxq(f64(xT)[:, unstriped(offs)], 0, "e4m3")
    h = gelu((mxq(f64(w1), 0, "e4m3").T @ xq) + f64(pos))
    return unpack_weight(w2_words, w2_scales).T @ mxq(h, 0, "e4m3")

@@ -1,0 +1,195 @@
+from contextlib import ExitStack
+
+import concourse.mybir as mybir
+
+K, T, S, H, N = 1024, 2048, 1024, 512, 128
+FLOPS = 2 * K * H * S + 2 * H * N * S
+
+F32 = mybir.dt.float32
+BF16 = mybir.dt.bfloat16
+I32 = mybir.dt.int32
+U32 = mybir.dt.uint32
+U16 = mybir.dt.uint16
+U8 = mybir.dt.uint8
+FP8X4 = mybir.dt.float8_e4m3fn_x4
+COPY = mybir.ActivationFunctionType.Copy
+GELU = mybir.ActivationFunctionType.Gelu_apprx_tanh
+ADD = mybir.AluOpType.add
+
+P = 128
+PACK = 4
+K_PASS = P * PACK
+PASSES = K // K_PASS
+HALF = 512
+X_CHUNKS = ((1024, 1024), (1024, 512, 256, 256))
+GROUPS = (128, 128, 256, 256, 128, 128)
+
+
+def tile_picked_embpos_gelu_e_kernel(tc, xT, w1, w2_words, w2_scales, pos, offs, out):
+    nc = tc.nc
+    with ExitStack() as ctx:
+        keep = ctx.enter_context(tc.tile_pool(name="keep", bufs=1))
+        psum = ctx.enter_context(tc.psum_pool(name="psum", bufs=1))
+
+        offsets = keep.tile([P, S // 16], U16, name="offsets")
+
+        x_raw = {}
+        for z in range(PASSES):
+            rows = xT[z * K_PASS:(z + 1) * K_PASS, :].rearrange("(p j) c -> p j c", j=PACK)
+            c0 = 0
+            for i, width in enumerate(X_CHUNKS[z]):
+                raw = keep.tile([P, PACK, width], F32, name="x_raw_%d_%d" % (z, i))
+                nc.sync.dma_start(out=raw[:], in_=rows[:, :, c0:c0 + width])
+                x_raw[z, i] = raw
+                c0 = c0 + width
+                if z == 0 and i == 0:
+                    nc.sync.dma_start(offsets[:], offs)
+        w_raw = []
+        for z in range(PASSES):
+            raw = keep.tile([P, PACK, H], F32, name="w_raw_%d" % z)
+            nc.sync.dma_start(out=raw[:], in_=w1[z * K_PASS:(z + 1) * K_PASS, :].rearrange("(p j) c -> p j c", j=PACK))
+            w_raw.append(raw)
+        pos_rows = pos.rearrange("(p t) s -> p t s", t=PACK)
+        pos_sb = []
+        for half in range(S // HALF):
+            raw = keep.tile([P, PACK, HALF], F32, name="pos_%d" % half)
+            nc.sync.dma_start(out=raw[:], in_=pos_rows[:, :, half * HALF:(half + 1) * HALF])
+            pos_sb.append(raw)
+
+        w2_codes = keep.tile([P, N], U32, name="w2_codes", align_bytes=64)
+        w2_bytes = keep.tile([P, N], U8, name="w2_bytes", align_bytes=64)
+        nc.gpsimd.memset(w2_bytes[:], 0)
+        for q in range(4):
+            nc.gpsimd.dma_start(out=w2_bytes[32 * q:32 * q + 4, :].bitcast(I32), in_=w2_scales[0, 4 * q:4 * q + 4, :].bitcast(I32))
+        nc.gpsimd.dma_start(out=w2_codes[:].bitcast(I32), in_=w2_words[0].rearrange("p n r -> p (n r)").bitcast(I32))
+
+        warm_in = keep.tile([P, 1], F32, name="warm_in")
+        warm_out = keep.tile([P, 1], F32, name="warm_out")
+        nc.vector.memset(warm_in[:], 0.0)
+        nc.scalar.activation(out=warm_out[:], in_=warm_in[:], func=GELU)
+
+        all_bytes = keep.tile([P, T], U8, name="all_bytes", align_bytes=64)
+        nc.vector.memset(all_bytes[:].bitcast(I32), 0)
+        all_words = [keep.tile([P, T], U32, name="all_words_%d" % z, align_bytes=64) for z in range(PASSES)]
+        got_words = {}
+        got_bytes = {}
+
+        def entries(half):
+            return offsets[:, half * (HALF // 16):(half + 1) * (HALF // 16)]
+
+        def gather_words(z, half, tag):
+            got = keep.tile([P, HALF], U32, name="got_words_%d_%d" % (z, half), tag=tag, align_bytes=64)
+            nc.vector.tensor_copy(out=got[:], in_=all_words[z][:].indirect(entries(half)))
+            got_words[z, half] = got
+
+        def gather_bytes(half, tag):
+            got = keep.tile([P, HALF], U8, name="got_bytes_%d" % half, tag=tag, align_bytes=64)
+            nc.vector.tensor_copy(out=got[:], in_=all_bytes[:].indirect(entries(half)))
+            got_bytes[half] = got
+
+        for z in range(PASSES):
+            c0 = 0
+            for i, width in enumerate(X_CHUNKS[z]):
+                raw = x_raw[z, i]
+                piece = min(width, 512)
+                for a in range(0, width, piece):
+                    xb = keep.tile([P, piece, PACK], BF16, name="x_bf_%d_%d_%d" % (z, i, a), align_bytes=64)
+                    cut = piece * 5 // 8
+                    nc.scalar.activation(
+                        out=xb[:, 0:cut, :].rearrange("p (c i) j -> p c j i", i=4),
+                        in_=raw[:, :, a:a + cut].rearrange("p j (c i) -> p c j i", i=4), func=COPY)
+                    nc.vector.tensor_copy(
+                        out=xb[:, cut:piece, :].rearrange("p (c i) j -> p c j i", i=4),
+                        in_=raw[:, :, a + cut:a + piece].rearrange("p j (c i) -> p c j i", i=4))
+                    nc.vector.quantize_mx(
+                        out=all_words[z][:, c0 + a:c0 + a + piece].bitcast(FP8X4),
+                        scales=all_bytes[4 * z:P, c0 + a:c0 + a + piece],
+                        in_=xb[:].rearrange("p c j -> p (c j)"))
+                c0 = c0 + width
+            if z == 0:
+                gather_words(0, 0, "got_words_0_0")
+                gather_words(0, 1, "got_words_0_1")
+
+        w_codes = []
+        w_bytes = []
+
+        def quantise_w1(z):
+            wb = keep.tile([P, PACK, P, PACK], BF16, name="w_bf_%d" % z, tag="w_bf_%d" % z, align_bytes=64)
+            nc.scalar.activation(
+                out=wb[:].rearrange("p t m j -> p m j t"),
+                in_=w_raw[z][:].rearrange("p j (m t) -> p m j t", t=PACK), func=COPY)
+            codes = keep.tile([P, H], U32, name="w_codes_%d" % z, align_bytes=64)
+            scales = keep.tile([P, H], U8, name="w_bytes_%d" % z, align_bytes=64)
+            nc.vector.quantize_mx(out=codes[:].bitcast(FP8X4), scales=scales[:], in_=wb[:].rearrange("p t m j -> p (t m j)"))
+            w_codes.append(codes)
+            w_bytes.append(scales)
+
+        banks = {}
+
+        def first_product(z, half):
+            for t in range(PACK):
+                if z == 0:
+                    banks[half, t] = psum.tile([P, HALF], F32, name="acc_%d_%d" % (half, t), tag="bank_%d" % (4 * half + t))
+                nc.tensor.matmul_mx(
+                    out=banks[half, t][:],
+                    lhsT=w_codes[z][:, t * P:(t + 1) * P].bitcast(FP8X4),
+                    lhsT_scale=w_bytes[z][:, t * P:(t + 1) * P],
+                    rhs=got_words[z, half][:].bitcast(FP8X4),
+                    rhs_scale=got_bytes[half][4 * z:P, :],
+                    start=(z == 0), stop=(z == PASSES - 1))
+
+        gather_bytes(0, "got_bytes_0")
+        gather_words(1, 0, "got_words_1_0")
+        gather_words(1, 1, "got_words_1_1")
+        quantise_w1(0)
+        first_product(0, 0)
+        quantise_w1(1)
+        first_product(1, 0)
+        gather_bytes(1, "w_bf_1")
+        first_product(0, 1)
+        first_product(1, 1)
+
+        starts = [sum(GROUPS[:g]) for g in range(len(GROUPS))]
+        pre = {}
+        hidden = {}
+        h_codes = {}
+        h_bytes = {}
+
+        def add_pos(g):
+            half, a = divmod(starts[g], HALF)
+            n = GROUPS[g]
+            pre[g] = keep.tile([P, PACK, n], F32, name="pre_%d" % g)
+            for t in range(PACK):
+                nc.vector.tensor_tensor(out=pre[g][:, t, :], in0=banks[half, t][:, a:a + n], in1=pos_sb[half][:, t, a:a + n], op=ADD)
+
+        def gelu(g):
+            n = GROUPS[g]
+            hidden[g] = keep.tile([P, n, PACK], BF16, name="hidden_%d" % g, align_bytes=64)
+            nc.scalar.activation(
+                out=hidden[g][:].rearrange("p (c i) t -> p c t i", i=4),
+                in_=pre[g][:].rearrange("p t (c i) -> p c t i", i=4), func=GELU)
+
+        def quantise_h(g):
+            n = GROUPS[g]
+            h_codes[g] = keep.tile([P, n], U32, name="h_codes_%d" % g, align_bytes=64)
+            h_bytes[g] = keep.tile([P, n], U8, name="h_bytes_%d" % g, align_bytes=64)
+            nc.vector.quantize_mx(out=h_codes[g][:].bitcast(FP8X4), scales=h_bytes[g][:], in_=hidden[g][:].rearrange("p c t -> p (c t)"))
+
+        def second_product(g):
+            n = GROUPS[g]
+            acc = psum.tile([P, n], F32, name="res_%d" % g, tag="bank_%d" % (g % 4))
+            nc.tensor.matmul_mx(out=acc[:], lhsT=w2_codes[:].bitcast(FP8X4), lhsT_scale=w2_bytes[:],
+                                rhs=h_codes[g][:].bitcast(FP8X4), rhs_scale=h_bytes[g][:], start=True, stop=True)
+            res = keep.tile([P, n], F32, name="res_sb_%d" % g)
+            nc.scalar.activation(out=res[:], in_=acc[:], func=COPY)
+            nc.sync.dma_start(out=out[:, starts[g]:starts[g] + n], in_=res[:])
+
+        last = len(GROUPS) - 1
+        for step in range(last + 4):
+            if step <= last:
+                add_pos(step)
+                gelu(step)
+            if 0 <= step - 1 <= last:
+                quantise_h(step - 1)
+            if 0 <= step - 3 <= last:
+                second_product(step - 3)

@@ -22,7 +22,10 @@ K_PASS = P * PACK
 PASSES = K // K_PASS
 HALF = 512
 X_CHUNKS = ((1024, 1024), (1024, 512, 256, 256))
-GROUPS = (128, 128, 256, 256, 128, 128)
+X_CUT = ((4, 3), (4, 4, 4, 4))
+W_CUT = (128, 80)
+GROUP = 128
+STORES = ((0, 1), (2, 3), (4, 5), (6,), (7,))
 
 
 def tile_picked_embpos_gelu_e_kernel(tc, xT, w1, w2_words, w2_scales, pos, offs, out):
@@ -49,19 +52,19 @@ def tile_picked_embpos_gelu_e_kernel(tc, xT, w1, w2_words, w2_scales, pos, offs,
             raw = keep.tile([P, PACK, H], F32, name="w_raw_%d" % z)
             nc.sync.dma_start(out=raw[:], in_=w1[z * K_PASS:(z + 1) * K_PASS, :].rearrange("(p j) c -> p j c", j=PACK))
             w_raw.append(raw)
+        w2_codes = keep.tile([P, N], U32, name="w2_codes", align_bytes=64)
+        w2_bytes = keep.tile([P, N], U8, name="w2_bytes", align_bytes=64)
+        nc.vector.memset(w2_bytes[:].bitcast(I32), 0)
+        for q in range(4):
+            nc.sync.dma_start(out=w2_bytes[32 * q:32 * q + 4, :].bitcast(I32), in_=w2_scales[0, 4 * q:4 * q + 4, :].bitcast(I32))
+        nc.sync.dma_start(out=w2_codes[:].bitcast(I32), in_=w2_words[0].rearrange("p n r -> p (n r)").bitcast(I32))
+
         pos_rows = pos.rearrange("(p t) s -> p t s", t=PACK)
         pos_sb = []
         for half in range(S // HALF):
             raw = keep.tile([P, PACK, HALF], F32, name="pos_%d" % half)
             nc.sync.dma_start(out=raw[:], in_=pos_rows[:, :, half * HALF:(half + 1) * HALF])
             pos_sb.append(raw)
-
-        w2_codes = keep.tile([P, N], U32, name="w2_codes", align_bytes=64)
-        w2_bytes = keep.tile([P, N], U8, name="w2_bytes", align_bytes=64)
-        nc.gpsimd.memset(w2_bytes[:], 0)
-        for q in range(4):
-            nc.gpsimd.dma_start(out=w2_bytes[32 * q:32 * q + 4, :].bitcast(I32), in_=w2_scales[0, 4 * q:4 * q + 4, :].bitcast(I32))
-        nc.gpsimd.dma_start(out=w2_codes[:].bitcast(I32), in_=w2_words[0].rearrange("p n r -> p (n r)").bitcast(I32))
 
         warm_in = keep.tile([P, 1], F32, name="warm_in")
         warm_out = keep.tile([P, 1], F32, name="warm_out")
@@ -91,10 +94,10 @@ def tile_picked_embpos_gelu_e_kernel(tc, xT, w1, w2_words, w2_scales, pos, offs,
             c0 = 0
             for i, width in enumerate(X_CHUNKS[z]):
                 raw = x_raw[z, i]
-                piece = min(width, 512)
-                for a in range(0, width, piece):
+                for a in range(0, width, 512):
+                    piece = min(width - a, 512)
                     xb = keep.tile([P, piece, PACK], BF16, name="x_bf_%d_%d_%d" % (z, i, a), align_bytes=64)
-                    cut = piece * 5 // 8
+                    cut = piece * X_CUT[z][i] // 8
                     nc.scalar.activation(
                         out=xb[:, 0:cut, :].rearrange("p (c i) j -> p c j i", i=4),
                         in_=raw[:, :, a:a + cut].rearrange("p j (c i) -> p c j i", i=4), func=COPY)
@@ -115,81 +118,81 @@ def tile_picked_embpos_gelu_e_kernel(tc, xT, w1, w2_words, w2_scales, pos, offs,
 
         def quantise_w1(z):
             wb = keep.tile([P, PACK, P, PACK], BF16, name="w_bf_%d" % z, tag="w_bf_%d" % z, align_bytes=64)
-            nc.scalar.activation(
-                out=wb[:].rearrange("p t m j -> p m j t"),
-                in_=w_raw[z][:].rearrange("p j (m t) -> p m j t", t=PACK), func=COPY)
+            dst = wb[:].rearrange("p t m j -> p m j t")
+            src = w_raw[z][:].rearrange("p j (m t) -> p m j t", t=PACK)
+            nc.scalar.activation(out=dst[:, 0:W_CUT[z]], in_=src[:, 0:W_CUT[z]], func=COPY)
+            if W_CUT[z] < P:
+                nc.vector.tensor_copy(out=dst[:, W_CUT[z]:P], in_=src[:, W_CUT[z]:P])
             codes = keep.tile([P, H], U32, name="w_codes_%d" % z, align_bytes=64)
             scales = keep.tile([P, H], U8, name="w_bytes_%d" % z, align_bytes=64)
             nc.vector.quantize_mx(out=codes[:].bitcast(FP8X4), scales=scales[:], in_=wb[:].rearrange("p t m j -> p (t m j)"))
             w_codes.append(codes)
             w_bytes.append(scales)
 
-        banks = {}
+        groups = S // GROUP
+        acc = [psum.tile([P, PACK, GROUP], F32, name="acc_%d" % g, tag="bank_%d" % g) for g in range(groups)]
 
-        def first_product(z, half):
-            for t in range(PACK):
-                if z == 0:
-                    banks[half, t] = psum.tile([P, HALF], F32, name="acc_%d_%d" % (half, t), tag="bank_%d" % (4 * half + t))
-                nc.tensor.matmul_mx(
-                    out=banks[half, t][:],
-                    lhsT=w_codes[z][:, t * P:(t + 1) * P].bitcast(FP8X4),
-                    lhsT_scale=w_bytes[z][:, t * P:(t + 1) * P],
-                    rhs=got_words[z, half][:].bitcast(FP8X4),
-                    rhs_scale=got_bytes[half][4 * z:P, :],
-                    start=(z == 0), stop=(z == PASSES - 1))
+        def product_pass(g, t, z):
+            half, a = divmod(g * GROUP, HALF)
+            nc.tensor.matmul_mx(
+                out=acc[g][:, t, :],
+                lhsT=w_codes[z][:, t * P:(t + 1) * P].bitcast(FP8X4),
+                lhsT_scale=w_bytes[z][:, t * P:(t + 1) * P],
+                rhs=got_words[z, half][:, a:a + GROUP].bitcast(FP8X4),
+                rhs_scale=got_bytes[half][4 * z:P, a:a + GROUP],
+                start=(z == 0), stop=(z == PASSES - 1))
 
         gather_bytes(0, "got_bytes_0")
+        gather_bytes(1, "got_bytes_1")
         gather_words(1, 0, "got_words_1_0")
-        gather_words(1, 1, "got_words_1_1")
         quantise_w1(0)
-        first_product(0, 0)
+        for g in range(groups):
+            product_pass(g, 0, 0)
         quantise_w1(1)
-        first_product(1, 0)
-        gather_bytes(1, "w_bf_1")
-        first_product(0, 1)
-        first_product(1, 1)
+        gather_words(1, 1, "w_bf_1")
+        for g in range(groups):
+            product_pass(g, 0, 1)
+            for t in range(1, PACK):
+                for z in range(PASSES):
+                    product_pass(g, t, z)
 
-        starts = [sum(GROUPS[:g]) for g in range(len(GROUPS))]
-        pre = {}
         hidden = {}
         h_codes = {}
         h_bytes = {}
 
-        def add_pos(g):
-            half, a = divmod(starts[g], HALF)
-            n = GROUPS[g]
-            pre[g] = keep.tile([P, PACK, n], F32, name="pre_%d" % g)
-            for t in range(PACK):
-                nc.vector.tensor_tensor(out=pre[g][:, t, :], in0=banks[half, t][:, a:a + n], in1=pos_sb[half][:, t, a:a + n], op=ADD)
-
-        def gelu(g):
-            n = GROUPS[g]
-            hidden[g] = keep.tile([P, n, PACK], BF16, name="hidden_%d" % g, align_bytes=64)
+        def add_pos_and_gelu(g):
+            half, a = divmod(g * GROUP, HALF)
+            pre = keep.tile([P, PACK, GROUP], F32, name="pre_%d" % g)
+            nc.vector.tensor_tensor(out=pre[:], in0=acc[g][:], in1=pos_sb[half][:, :, a:a + GROUP], op=ADD)
+            hidden[g] = keep.tile([P, GROUP, PACK], BF16, name="hidden_%d" % g, align_bytes=64)
             nc.scalar.activation(
                 out=hidden[g][:].rearrange("p (c i) t -> p c t i", i=4),
-                in_=pre[g][:].rearrange("p t (c i) -> p c t i", i=4), func=GELU)
+                in_=pre[:].rearrange("p t (c i) -> p c t i", i=4), func=GELU)
 
         def quantise_h(g):
-            n = GROUPS[g]
-            h_codes[g] = keep.tile([P, n], U32, name="h_codes_%d" % g, align_bytes=64)
-            h_bytes[g] = keep.tile([P, n], U8, name="h_bytes_%d" % g, align_bytes=64)
+            h_codes[g] = keep.tile([P, GROUP], U32, name="h_codes_%d" % g, align_bytes=64)
+            h_bytes[g] = keep.tile([P, GROUP], U8, name="h_bytes_%d" % g, align_bytes=64)
             nc.vector.quantize_mx(out=h_codes[g][:].bitcast(FP8X4), scales=h_bytes[g][:], in_=hidden[g][:].rearrange("p c t -> p (c t)"))
 
-        def second_product(g):
-            n = GROUPS[g]
-            acc = psum.tile([P, n], F32, name="res_%d" % g, tag="bank_%d" % (g % 4))
-            nc.tensor.matmul_mx(out=acc[:], lhsT=w2_codes[:].bitcast(FP8X4), lhsT_scale=w2_bytes[:],
-                                rhs=h_codes[g][:].bitcast(FP8X4), rhs_scale=h_bytes[g][:], start=True, stop=True)
-            res = keep.tile([P, n], F32, name="res_sb_%d" % g)
-            nc.scalar.activation(out=res[:], in_=acc[:], func=COPY)
-            nc.sync.dma_start(out=out[:, starts[g]:starts[g] + n], in_=res[:])
+        def second_product(members):
+            n = GROUP * len(members)
+            first = members[0]
+            sums = psum.tile([P, n], F32, name="sums_%d" % first, tag="bank_%d" % (first % 6))
+            for i, g in enumerate(members):
+                nc.tensor.matmul_mx(out=sums[:, i * GROUP:(i + 1) * GROUP], lhsT=w2_codes[:].bitcast(FP8X4), lhsT_scale=w2_bytes[:],
+                                    rhs=h_codes[g][:].bitcast(FP8X4), rhs_scale=h_bytes[g][:], start=True, stop=True)
+            res = keep.tile([P, n], F32, name="res_%d" % first)
+            if first == groups - 2:
+                nc.vector.tensor_copy(out=res[:], in_=sums[:])
+            else:
+                nc.scalar.activation(out=res[:], in_=sums[:], func=COPY)
+            nc.sync.dma_start(out=out[:, first * GROUP:first * GROUP + n], in_=res[:])
 
-        last = len(GROUPS) - 1
-        for step in range(last + 4):
-            if step <= last:
-                add_pos(step)
-                gelu(step)
-            if 0 <= step - 1 <= last:
+        for step in range(groups + 1):
+            if step < groups:
+                add_pos_and_gelu(step)
+            if step >= 1:
                 quantise_h(step - 1)
-            if 0 <= step - 3 <= last:
-                second_product(step - 3)
+                for members in STORES:
+                    if members[-1] == step - 1:
+                        second_product(members)

@@ -22,10 +22,11 @@ K_PASS = P * PACK
 PASSES = K // K_PASS
 HALF = 512
 X_CHUNKS = ((1024, 1024), (1024, 512, 256, 256))
-X_CUT = ((4, 3), (4, 4, 4, 4))
+X_CUT = ((4, 3), (4, 4, 4, 3))
 W_CUT = (128, 80)
 GROUP = 128
-STORES = ((0, 1), (2, 3), (4, 5), (6,), (7,))
+RUNS = ((0, 1), (2, 3), (4, 5), (6,), (7,))
+RING = 4
 
 
 def tile_picked_embpos_gelu_e_kernel(tc, xT, w1, w2_words, w2_scales, pos, offs, out):
@@ -65,11 +66,6 @@ def tile_picked_embpos_gelu_e_kernel(tc, xT, w1, w2_words, w2_scales, pos, offs,
             raw = keep.tile([P, PACK, HALF], F32, name="pos_%d" % half)
             nc.sync.dma_start(out=raw[:], in_=pos_rows[:, :, half * HALF:(half + 1) * HALF])
             pos_sb.append(raw)
-
-        warm_in = keep.tile([P, 1], F32, name="warm_in")
-        warm_out = keep.tile([P, 1], F32, name="warm_out")
-        nc.vector.memset(warm_in[:], 0.0)
-        nc.scalar.activation(out=warm_out[:], in_=warm_in[:], func=GELU)
 
         all_bytes = keep.tile([P, T], U8, name="all_bytes", align_bytes=64)
         nc.vector.memset(all_bytes[:].bitcast(I32), 0)
@@ -130,10 +126,12 @@ def tile_picked_embpos_gelu_e_kernel(tc, xT, w1, w2_words, w2_scales, pos, offs,
             w_bytes.append(scales)
 
         groups = S // GROUP
-        acc = [psum.tile([P, PACK, GROUP], F32, name="acc_%d" % g, tag="bank_%d" % g) for g in range(groups)]
+        acc = {}
 
         def product_pass(g, t, z):
             half, a = divmod(g * GROUP, HALF)
+            if t == 0 and z == 0:
+                acc[g] = psum.tile([P, PACK, GROUP], F32, name="acc_%d" % g, tag="bank_%d" % (g % RING))
             nc.tensor.matmul_mx(
                 out=acc[g][:, t, :],
                 lhsT=w_codes[z][:, t * P:(t + 1) * P].bitcast(FP8X4),
@@ -144,55 +142,60 @@ def tile_picked_embpos_gelu_e_kernel(tc, xT, w1, w2_words, w2_scales, pos, offs,
 
         gather_bytes(0, "got_bytes_0")
         gather_bytes(1, "got_bytes_1")
+        idle = psum.tile([P, HALF], F32, name="idle", tag="bank_7")
+        for i in range(4):
+            nc.tensor.matmul_mx(out=idle[:], lhsT=got_words[0, 0][:, 0:P].bitcast(FP8X4), lhsT_scale=got_bytes[0][:, 0:P],
+                                rhs=got_words[0, 1][:].bitcast(FP8X4), rhs_scale=got_bytes[1][:], start=True, stop=True)
         gather_words(1, 0, "got_words_1_0")
         quantise_w1(0)
-        for g in range(groups):
+        for g in range(RING):
             product_pass(g, 0, 0)
         quantise_w1(1)
         gather_words(1, 1, "w_bf_1")
-        for g in range(groups):
+
+        def finish_first_product(g):
+            if g >= RING:
+                product_pass(g, 0, 0)
             product_pass(g, 0, 1)
             for t in range(1, PACK):
                 for z in range(PASSES):
                     product_pass(g, t, z)
 
         hidden = {}
-        h_codes = {}
-        h_bytes = {}
 
-        def add_pos_and_gelu(g):
+        def add_pos_and_gelu(r, i):
+            g = RUNS[r][i]
             half, a = divmod(g * GROUP, HALF)
             pre = keep.tile([P, PACK, GROUP], F32, name="pre_%d" % g)
             nc.vector.tensor_tensor(out=pre[:], in0=acc[g][:], in1=pos_sb[half][:, :, a:a + GROUP], op=ADD)
-            hidden[g] = keep.tile([P, GROUP, PACK], BF16, name="hidden_%d" % g, align_bytes=64)
+            if i == 0:
+                hidden[r] = keep.tile([P, GROUP * len(RUNS[r]), PACK], BF16, name="hidden_%d" % r, align_bytes=64)
             nc.scalar.activation(
-                out=hidden[g][:].rearrange("p (c i) t -> p c t i", i=4),
+                out=hidden[r][:, i * GROUP:(i + 1) * GROUP, :].rearrange("p (c i) t -> p c t i", i=4),
                 in_=pre[:].rearrange("p t (c i) -> p c t i", i=4), func=GELU)
 
-        def quantise_h(g):
-            h_codes[g] = keep.tile([P, GROUP], U32, name="h_codes_%d" % g, align_bytes=64)
-            h_bytes[g] = keep.tile([P, GROUP], U8, name="h_bytes_%d" % g, align_bytes=64)
-            nc.vector.quantize_mx(out=h_codes[g][:].bitcast(FP8X4), scales=h_bytes[g][:], in_=hidden[g][:].rearrange("p c t -> p (c t)"))
+        def second_product(r):
+            s0 = RUNS[r][0] * GROUP
+            n = GROUP * len(RUNS[r])
+            h_codes = keep.tile([P, n], U32, name="h_codes_%d" % r, align_bytes=64)
+            h_bytes = keep.tile([P, n], U8, name="h_bytes_%d" % r, align_bytes=64)
+            nc.vector.quantize_mx(out=h_codes[:].bitcast(FP8X4), scales=h_bytes[:], in_=hidden[r][:].rearrange("p c t -> p (c t)"))
+            sums = psum.tile([P, n], F32, name="sums_%d" % r, tag="bank_%d" % (RING + r % (8 - RING)))
+            nc.tensor.matmul_mx(out=sums[:], lhsT=w2_codes[:].bitcast(FP8X4), lhsT_scale=w2_bytes[:],
+                                rhs=h_codes[:].bitcast(FP8X4), rhs_scale=h_bytes[:], start=True, stop=True)
+            res = keep.tile([P, n], F32, name="res_%d" % r)
+            nc.scalar.activation(out=res[:], in_=sums[:], func=COPY)
+            queue = nc.scalar if r == len(RUNS) - 1 else nc.sync
+            queue.dma_start(out=out[:, s0:s0 + n], in_=res[:])
 
-        def second_product(members):
-            n = GROUP * len(members)
-            first = members[0]
-            sums = psum.tile([P, n], F32, name="sums_%d" % first, tag="bank_%d" % (first % 6))
-            for i, g in enumerate(members):
-                nc.tensor.matmul_mx(out=sums[:, i * GROUP:(i + 1) * GROUP], lhsT=w2_codes[:].bitcast(FP8X4), lhsT_scale=w2_bytes[:],
-                                    rhs=h_codes[g][:].bitcast(FP8X4), rhs_scale=h_bytes[g][:], start=True, stop=True)
-            res = keep.tile([P, n], F32, name="res_%d" % first)
-            if first == groups - 2:
-                nc.vector.tensor_copy(out=res[:], in_=sums[:])
-            else:
-                nc.scalar.activation(out=res[:], in_=sums[:], func=COPY)
-            nc.sync.dma_start(out=out[:, first * GROUP:first * GROUP + n], in_=res[:])
-
-        for step in range(groups + 1):
-            if step < groups:
-                add_pos_and_gelu(step)
-            if step >= 1:
-                quantise_h(step - 1)
-                for members in STORES:
-                    if members[-1] == step - 1:
-                        second_product(members)
+        for g in range(RING):
+            finish_first_product(g)
+        for g in range(groups + 1):
+            for r, run in enumerate(RUNS):
+                if g in run:
+                    add_pos_and_gelu(r, run.index(g))
+            for r, run in enumerate(RUNS):
+                if run[-1] == g - 1:
+                    second_product(r)
+            if g + RING < groups:
+                finish_first_product(g + RING)

@@ -21,9 +21,10 @@ PACK = 4
 K_PASS = P * PACK
 PASSES = K // K_PASS
 HALF = 512
-X_CHUNKS = ((1024, 1024), (1024, 512, 256, 256))
-X_CUT = ((4, 3), (4, 4, 4, 3))
-W_CUT = (128, 80)
+X_CHUNKS = ((1024, 512, 512), (512, 512, 256, 256, 256, 128, 128))
+X_CUT = ((4, 4, 3), (8, 5, 6, 6, 6, 6, 5))
+W_PIECES = 2
+W_CALLS = (1, 2)
 GROUP = 128
 RUNS = ((0, 1), (2, 3), (4, 5), (6,), (7,))
 RING = 4
@@ -48,11 +49,13 @@ def tile_picked_embpos_gelu_e_kernel(tc, xT, w1, w2_words, w2_scales, pos, offs,
                 c0 = c0 + width
                 if z == 0 and i == 0:
                     nc.sync.dma_start(offsets[:], offs)
-        w_raw = []
+        w_raw = {}
         for z in range(PASSES):
-            raw = keep.tile([P, PACK, H], F32, name="w_raw_%d" % z)
-            nc.sync.dma_start(out=raw[:], in_=w1[z * K_PASS:(z + 1) * K_PASS, :].rearrange("(p j) c -> p j c", j=PACK))
-            w_raw.append(raw)
+            rows = w1[z * K_PASS:(z + 1) * K_PASS, :].rearrange("(p j) c -> p j c", j=PACK)
+            for i in range(W_PIECES):
+                raw = keep.tile([P, PACK, H // W_PIECES], F32, name="w_raw_%d_%d" % (z, i))
+                nc.sync.dma_start(out=raw[:], in_=rows[:, :, i * (H // W_PIECES):(i + 1) * (H // W_PIECES)])
+                w_raw[z, i] = raw
         w2_codes = keep.tile([P, N], U32, name="w2_codes", align_bytes=64)
         w2_bytes = keep.tile([P, N], U8, name="w2_bytes", align_bytes=64)
         nc.vector.memset(w2_bytes[:].bitcast(I32), 0)
@@ -76,10 +79,12 @@ def tile_picked_embpos_gelu_e_kernel(tc, xT, w1, w2_words, w2_scales, pos, offs,
         def entries(half):
             return offsets[:, half * (HALF // 16):(half + 1) * (HALF // 16)]
 
-        def gather_words(z, half, tag):
-            got = keep.tile([P, HALF], U32, name="got_words_%d_%d" % (z, half), tag=tag, align_bytes=64)
-            nc.vector.tensor_copy(out=got[:], in_=all_words[z][:].indirect(entries(half)))
-            got_words[z, half] = got
+        def gather_words(z, s0, n, tag):
+            got = keep.tile([P, n], U32, name="got_words_%d_%d" % (z, s0), tag=tag, align_bytes=64)
+            nc.vector.tensor_copy(out=got[:], in_=all_words[z][:].indirect(offsets[:, s0 // 16:(s0 + n) // 16]))
+            for g in range(s0 // GROUP, (s0 + n) // GROUP):
+                got_words[z, g] = got[:, g * GROUP - s0:(g + 1) * GROUP - s0]
+            return got
 
         def gather_bytes(half, tag):
             got = keep.tile([P, HALF], U8, name="got_bytes_%d" % half, tag=tag, align_bytes=64)
@@ -97,17 +102,18 @@ def tile_picked_embpos_gelu_e_kernel(tc, xT, w1, w2_words, w2_scales, pos, offs,
                     nc.scalar.activation(
                         out=xb[:, 0:cut, :].rearrange("p (c i) j -> p c j i", i=4),
                         in_=raw[:, :, a:a + cut].rearrange("p j (c i) -> p c j i", i=4), func=COPY)
-                    nc.vector.tensor_copy(
-                        out=xb[:, cut:piece, :].rearrange("p (c i) j -> p c j i", i=4),
-                        in_=raw[:, :, a + cut:a + piece].rearrange("p j (c i) -> p c j i", i=4))
+                    if cut < piece:
+                        nc.vector.tensor_copy(
+                            out=xb[:, cut:piece, :].rearrange("p (c i) j -> p c j i", i=4),
+                            in_=raw[:, :, a + cut:a + piece].rearrange("p j (c i) -> p c j i", i=4))
                     nc.vector.quantize_mx(
                         out=all_words[z][:, c0 + a:c0 + a + piece].bitcast(FP8X4),
                         scales=all_bytes[4 * z:P, c0 + a:c0 + a + piece],
                         in_=xb[:].rearrange("p c j -> p (c j)"))
                 c0 = c0 + width
             if z == 0:
-                gather_words(0, 0, "got_words_0_0")
-                gather_words(0, 1, "got_words_0_1")
+                gather_words(0, 0, HALF, "got_words_0_0")
+                early = gather_words(0, HALF, HALF, "got_words_0_1")
 
         w_codes = []
         w_bytes = []
@@ -115,13 +121,15 @@ def tile_picked_embpos_gelu_e_kernel(tc, xT, w1, w2_words, w2_scales, pos, offs,
         def quantise_w1(z):
             wb = keep.tile([P, PACK, P, PACK], BF16, name="w_bf_%d" % z, tag="w_bf_%d" % z, align_bytes=64)
             dst = wb[:].rearrange("p t m j -> p m j t")
-            src = w_raw[z][:].rearrange("p j (m t) -> p m j t", t=PACK)
-            nc.scalar.activation(out=dst[:, 0:W_CUT[z]], in_=src[:, 0:W_CUT[z]], func=COPY)
-            if W_CUT[z] < P:
-                nc.vector.tensor_copy(out=dst[:, W_CUT[z]:P], in_=src[:, W_CUT[z]:P])
+            for i in range(W_PIECES):
+                src = w_raw[z, i][:].rearrange("p j (m t) -> p m j t", t=PACK)
+                nc.scalar.activation(out=dst[:, i * (P // W_PIECES):(i + 1) * (P // W_PIECES)], in_=src, func=COPY)
             codes = keep.tile([P, H], U32, name="w_codes_%d" % z, align_bytes=64)
             scales = keep.tile([P, H], U8, name="w_bytes_%d" % z, align_bytes=64)
-            nc.vector.quantize_mx(out=codes[:].bitcast(FP8X4), scales=scales[:], in_=wb[:].rearrange("p t m j -> p (t m j)"))
+            step = H // W_CALLS[z]
+            for c in range(0, H, step):
+                nc.vector.quantize_mx(out=codes[:, c:c + step].bitcast(FP8X4), scales=scales[:, c:c + step],
+                                      in_=wb[:].rearrange("p t m j -> p (t m j)")[:, PACK * c:PACK * (c + step)])
             w_codes.append(codes)
             w_bytes.append(scales)
 
@@ -136,7 +144,7 @@ def tile_picked_embpos_gelu_e_kernel(tc, xT, w1, w2_words, w2_scales, pos, offs,
                 out=acc[g][:, t, :],
                 lhsT=w_codes[z][:, t * P:(t + 1) * P].bitcast(FP8X4),
                 lhsT_scale=w_bytes[z][:, t * P:(t + 1) * P],
-                rhs=got_words[z, half][:, a:a + GROUP].bitcast(FP8X4),
+                rhs=got_words[z, g].bitcast(FP8X4),
                 rhs_scale=got_bytes[half][4 * z:P, a:a + GROUP],
                 start=(z == 0), stop=(z == PASSES - 1))
 
@@ -144,14 +152,15 @@ def tile_picked_embpos_gelu_e_kernel(tc, xT, w1, w2_words, w2_scales, pos, offs,
         gather_bytes(1, "got_bytes_1")
         idle = psum.tile([P, HALF], F32, name="idle", tag="bank_7")
         for i in range(4):
-            nc.tensor.matmul_mx(out=idle[:], lhsT=got_words[0, 0][:, 0:P].bitcast(FP8X4), lhsT_scale=got_bytes[0][:, 0:P],
-                                rhs=got_words[0, 1][:].bitcast(FP8X4), rhs_scale=got_bytes[1][:], start=True, stop=True)
-        gather_words(1, 0, "got_words_1_0")
+            nc.tensor.matmul_mx(out=idle[:], lhsT=got_words[0, 0].bitcast(FP8X4), lhsT_scale=got_bytes[0][:, 0:P],
+                                rhs=early[:].bitcast(FP8X4), rhs_scale=got_bytes[1][:], start=True, stop=True)
+        gather_words(1, 0, 512, "got_words_1_0")
+        gather_words(1, 512, 256, "got_words_1_1")
         quantise_w1(0)
         for g in range(RING):
             product_pass(g, 0, 0)
         quantise_w1(1)
-        gather_words(1, 1, "w_bf_1")
+        gather_words(1, 768, 256, "w_bf_1")
 
         def finish_first_product(g):
             if g >= RING:

@@ -24,6 +24,7 @@ HALF = 512
 X_CHUNKS = ((1024, 512, 512), (512, 512, 256, 256, 256, 128, 128))
 X_CUT = ((4, 4, 3), (8, 5, 6, 6, 6, 6, 5))
 W_PIECES = 2
+POS_CHUNKS = (256, 256, 256, 256)
 W_CALLS = (1, 2)
 GROUP = 128
 RUNS = ((0, 1), (2, 3), (4, 5), (6,), (7,))
@@ -65,10 +66,13 @@ def tile_picked_embpos_gelu_e_kernel(tc, xT, w1, w2_words, w2_scales, pos, offs,
 
         pos_rows = pos.rearrange("(p t) s -> p t s", t=PACK)
         pos_sb = []
-        for half in range(S // HALF):
-            raw = keep.tile([P, PACK, HALF], F32, name="pos_%d" % half)
-            nc.sync.dma_start(out=raw[:], in_=pos_rows[:, :, half * HALF:(half + 1) * HALF])
-            pos_sb.append(raw)
+        s0 = 0
+        for width in POS_CHUNKS:
+            raw = keep.tile([P, PACK, width], F32, name="pos_%d" % s0, tag="pos_%d" % s0, align_bytes=64)
+            nc.sync.dma_start(out=raw[:], in_=pos_rows[:, :, s0:s0 + width])
+            for a in range(0, width, GROUP):
+                pos_sb.append(raw[:, :, a:a + GROUP])
+            s0 = s0 + width
 
         all_bytes = keep.tile([P, T], U8, name="all_bytes", align_bytes=64)
         nc.vector.memset(all_bytes[:].bitcast(I32), 0)
@@ -171,14 +175,14 @@ def tile_picked_embpos_gelu_e_kernel(tc, xT, w1, w2_words, w2_scales, pos, offs,
                     product_pass(g, t, z)
 
         hidden = {}
+        h_tiles = []
 
         def add_pos_and_gelu(r, i):
             g = RUNS[r][i]
-            half, a = divmod(g * GROUP, HALF)
             pre = keep.tile([P, PACK, GROUP], F32, name="pre_%d" % g)
-            nc.vector.tensor_tensor(out=pre[:], in0=acc[g][:], in1=pos_sb[half][:, :, a:a + GROUP], op=ADD)
+            nc.vector.tensor_tensor(out=pre[:], in0=acc[g][:], in1=pos_sb[g], op=ADD)
             if i == 0:
-                hidden[r] = keep.tile([P, GROUP * len(RUNS[r]), PACK], BF16, name="hidden_%d" % r, align_bytes=64)
+                hidden[r] = keep.tile([P, GROUP * len(RUNS[r]), PACK], BF16, name="hidden_%d" % r, tag="hidden_%d" % r, align_bytes=64)
             nc.scalar.activation(
                 out=hidden[r][:, i * GROUP:(i + 1) * GROUP, :].rearrange("p (c i) t -> p c t i", i=4),
                 in_=pre[:].rearrange("p t (c i) -> p c t i", i=4), func=GELU)
@@ -186,25 +190,35 @@ def tile_picked_embpos_gelu_e_kernel(tc, xT, w1, w2_words, w2_scales, pos, offs,
         def second_product(r):
             s0 = RUNS[r][0] * GROUP
             n = GROUP * len(RUNS[r])
-            h_codes = keep.tile([P, n], U32, name="h_codes_%d" % r, align_bytes=64)
+            if r == 0:
+                h_tiles.append(keep.tile([P, n], U32, name="h_codes_first", tag="pos_512", align_bytes=64))
+                h_codes = h_tiles[0][:]
+            else:
+                if r == 1:
+                    h_tiles.append(keep.tile([P, S], U32, name="h_codes_rest", tag="pos_768", align_bytes=64))
+                h_codes = h_tiles[1][:, s0:s0 + n]
             h_bytes = keep.tile([P, n], U8, name="h_bytes_%d" % r, align_bytes=64)
-            nc.vector.quantize_mx(out=h_codes[:].bitcast(FP8X4), scales=h_bytes[:], in_=hidden[r][:].rearrange("p c t -> p (c t)"))
+            nc.vector.quantize_mx(out=h_codes.bitcast(FP8X4), scales=h_bytes[:], in_=hidden[r][:].rearrange("p c t -> p (c t)"))
             sums = psum.tile([P, n], F32, name="sums_%d" % r, tag="bank_%d" % (RING + r % (8 - RING)))
             nc.tensor.matmul_mx(out=sums[:], lhsT=w2_codes[:].bitcast(FP8X4), lhsT_scale=w2_bytes[:],
-                                rhs=h_codes[:].bitcast(FP8X4), rhs_scale=h_bytes[:], start=True, stop=True)
+                                rhs=h_codes.bitcast(FP8X4), rhs_scale=h_bytes[:], start=True, stop=True)
             res = keep.tile([P, n], F32, name="res_%d" % r)
-            nc.scalar.activation(out=res[:], in_=sums[:], func=COPY)
+            if r == 2:
+                nc.vector.tensor_copy(out=res[:], in_=sums[:])
+            else:
+                nc.scalar.activation(out=res[:], in_=sums[:], func=COPY)
             queue = nc.scalar if r == len(RUNS) - 1 else nc.sync
             queue.dma_start(out=out[:, s0:s0 + n], in_=res[:])
 
         for g in range(RING):
             finish_first_product(g)
-        for g in range(groups + 1):
+        for g in range(groups):
             for r, run in enumerate(RUNS):
                 if g in run:
                     add_pos_and_gelu(r, run.index(g))
-            for r, run in enumerate(RUNS):
-                if run[-1] == g - 1:
-                    second_product(r)
             if g + RING < groups:
                 finish_first_product(g + RING)
+            if g == 5:
+                second_product(0)
+        for r in range(1, len(RUNS)):
+            second_product(r)

@@ -21,9 +21,9 @@ PACK = 4
 K_PASS = P * PACK
 PASSES = K // K_PASS
 HALF = 512
-X_CHUNKS = ((1024, 512, 512), (512, 512, 256, 256, 256, 128, 128))
-X_CUT = ((4, 4, 3), (8, 5, 6, 6, 6, 6, 5))
-W_PIECES = 2
+X_CHUNKS = ((1024, 512, 512), (512, 512, 512, 256, 128, 128))
+X_CUT = ((4, 4, 3), (8, 5, 4, 5, 6, 5))
+W_CHUNKS = ((256, 256), (256, 128, 128))
 POS_CHUNKS = (256, 256, 256, 256)
 W_CALLS = (1, 2)
 GROUP = 128
@@ -53,10 +53,12 @@ def tile_picked_embpos_gelu_e_kernel(tc, xT, w1, w2_words, w2_scales, pos, offs,
         w_raw = {}
         for z in range(PASSES):
             rows = w1[z * K_PASS:(z + 1) * K_PASS, :].rearrange("(p j) c -> p j c", j=PACK)
-            for i in range(W_PIECES):
-                raw = keep.tile([P, PACK, H // W_PIECES], F32, name="w_raw_%d_%d" % (z, i))
-                nc.sync.dma_start(out=raw[:], in_=rows[:, :, i * (H // W_PIECES):(i + 1) * (H // W_PIECES)])
+            c0 = 0
+            for i, width in enumerate(W_CHUNKS[z]):
+                raw = keep.tile([P, PACK, width], F32, name="w_raw_%d_%d" % (z, i))
+                nc.sync.dma_start(out=raw[:], in_=rows[:, :, c0:c0 + width])
                 w_raw[z, i] = raw
+                c0 = c0 + width
         w2_codes = keep.tile([P, N], U32, name="w2_codes", align_bytes=64)
         w2_bytes = keep.tile([P, N], U8, name="w2_bytes", align_bytes=64)
         nc.vector.memset(w2_bytes[:].bitcast(I32), 0)
@@ -125,9 +127,11 @@ def tile_picked_embpos_gelu_e_kernel(tc, xT, w1, w2_words, w2_scales, pos, offs,
         def quantise_w1(z):
             wb = keep.tile([P, PACK, P, PACK], BF16, name="w_bf_%d" % z, tag="w_bf_%d" % z, align_bytes=64)
             dst = wb[:].rearrange("p t m j -> p m j t")
-            for i in range(W_PIECES):
+            m0 = 0
+            for i, width in enumerate(W_CHUNKS[z]):
                 src = w_raw[z, i][:].rearrange("p j (m t) -> p m j t", t=PACK)
-                nc.scalar.activation(out=dst[:, i * (P // W_PIECES):(i + 1) * (P // W_PIECES)], in_=src, func=COPY)
+                nc.scalar.activation(out=dst[:, m0:m0 + width // PACK], in_=src, func=COPY)
+                m0 = m0 + width // PACK
             codes = keep.tile([P, H], U32, name="w_codes_%d" % z, align_bytes=64)
             scales = keep.tile([P, H], U8, name="w_bytes_%d" % z, align_bytes=64)
             step = H // W_CALLS[z]
@@ -155,11 +159,17 @@ def tile_picked_embpos_gelu_e_kernel(tc, xT, w1, w2_words, w2_scales, pos, offs,
         gather_bytes(0, "got_bytes_0")
         gather_bytes(1, "got_bytes_1")
         idle = psum.tile([P, HALF], F32, name="idle", tag="bank_7")
-        for i in range(4):
-            nc.tensor.matmul_mx(out=idle[:], lhsT=got_words[0, 0].bitcast(FP8X4), lhsT_scale=got_bytes[0][:, 0:P],
+
+        def warm_up(stationary):
+            nc.tensor.matmul_mx(out=idle[:], lhsT=stationary.bitcast(FP8X4), lhsT_scale=got_bytes[0][:, 0:P],
                                 rhs=early[:].bitcast(FP8X4), rhs_scale=got_bytes[1][:], start=True, stop=True)
+
+        warm_up(got_words[0, 0])
+        warm_up(got_words[0, 0])
         gather_words(1, 0, 512, "got_words_1_0")
+        warm_up(got_words[1, 0])
         gather_words(1, 512, 256, "got_words_1_1")
+        warm_up(got_words[1, 4])
         quantise_w1(0)
         for g in range(RING):
             product_pass(g, 0, 0)

@@ -21,41 +21,53 @@ PACK = 4
 K_PASS = P * PACK
 PASSES = K // K_PASS
 HALF = 512
-X_CHUNKS = ((1024, 512, 512), (512, 512, 512, 256, 128, 128))
-X_CUT = ((4, 4, 3), (8, 5, 4, 5, 6, 5))
+X_LOADS = (
+    ((2048, 704),),
+    ((1024, 1024), (768, 0), (256, 256)),
+    ((512, 512), (512, 512), (512, 512), (512, 512)),
+    ((768, 768), (768, 512), (256, 0), (256, 128)),
+)
+W_SHARE = 0
 W_CHUNKS = ((256, 256), (256, 128, 128))
 POS_CHUNKS = (256, 256, 256, 256)
 W_CALLS = (1, 2)
 GROUP = 128
-RUNS = ((0, 1), (2, 3), (4, 5), (6,), (7,))
 RING = 4
+RUNS = ((0, 1), (2, 3), (4, 5), (6,), (7,))
 
 
 def tile_picked_embpos_gelu_e_kernel(tc, xT, w1, w2_words, w2_scales, pos, offs, out):
     nc = tc.nc
     with ExitStack() as ctx:
         keep = ctx.enter_context(tc.tile_pool(name="keep", bufs=1))
+        held = ctx.enter_context(tc.tile_pool(name="held", bufs=1))
         psum = ctx.enter_context(tc.psum_pool(name="psum", bufs=1))
 
         offsets = keep.tile([P, S // 16], U16, name="offsets")
 
         x_raw = {}
-        for z in range(PASSES):
+        for pair, loads in enumerate(X_LOADS):
+            z, u = divmod(pair, 2)
             rows = xT[z * K_PASS:(z + 1) * K_PASS, :].rearrange("(p j) c -> p j c", j=PACK)
             c0 = 0
-            for i, width in enumerate(X_CHUNKS[z]):
-                raw = keep.tile([P, PACK, width], F32, name="x_raw_%d_%d" % (z, i))
-                nc.sync.dma_start(out=raw[:], in_=rows[:, :, c0:c0 + width])
-                x_raw[z, i] = raw
+            for i, (width, cut) in enumerate(loads):
+                raw = keep.tile([P, 2, width], F32, name="x_raw_%d_%d" % (pair, i))
+                nc.sync.dma_start(out=raw[:], in_=rows[:, 2 * u:2 * u + 2, c0:c0 + width])
+                x_raw[pair, i] = raw
                 c0 = c0 + width
-                if z == 0 and i == 0:
-                    nc.sync.dma_start(offsets[:], offs)
+            if pair == 0:
+                nc.sync.dma_start(offsets[:], offs)
         w_raw = {}
         for z in range(PASSES):
             rows = w1[z * K_PASS:(z + 1) * K_PASS, :].rearrange("(p j) c -> p j c", j=PACK)
             c0 = 0
             for i, width in enumerate(W_CHUNKS[z]):
-                raw = keep.tile([P, PACK, width], F32, name="w_raw_%d_%d" % (z, i))
+                if (z, i) == (0, 1):
+                    raw = held.tile([P, PACK, width], F32, name="w_raw_0_last", offset=4096, align_bytes=64)
+                elif (z, i) == (1, 2):
+                    raw = held.tile([P, PACK, width], F32, name="w_raw_1_last", offset=8192, align_bytes=64)
+                else:
+                    raw = keep.tile([P, PACK, width], F32, name="w_raw_%d_%d" % (z, i))
                 nc.sync.dma_start(out=raw[:], in_=rows[:, :, c0:c0 + width])
                 w_raw[z, i] = raw
                 c0 = c0 + width
@@ -76,50 +88,57 @@ def tile_picked_embpos_gelu_e_kernel(tc, xT, w1, w2_words, w2_scales, pos, offs,
                 pos_sb.append(raw[:, :, a:a + GROUP])
             s0 = s0 + width
 
-        all_bytes = keep.tile([P, T], U8, name="all_bytes", align_bytes=64)
-        nc.vector.memset(all_bytes[:].bitcast(I32), 0)
-        all_words = [keep.tile([P, T], U32, name="all_words_%d" % z, align_bytes=64) for z in range(PASSES)]
-        got_words = {}
-        got_bytes = {}
+        got = {}
+        woven = {}
+        x_codes = {}
+        x_bytes = {}
 
-        def entries(half):
-            return offsets[:, half * (HALF // 16):(half + 1) * (HALF // 16)]
-
-        def gather_words(z, s0, n, tag):
-            got = keep.tile([P, n], U32, name="got_words_%d_%d" % (z, s0), tag=tag, align_bytes=64)
-            nc.vector.tensor_copy(out=got[:], in_=all_words[z][:].indirect(offsets[:, s0 // 16:(s0 + n) // 16]))
-            for g in range(s0 // GROUP, (s0 + n) // GROUP):
-                got_words[z, g] = got[:, g * GROUP - s0:(g + 1) * GROUP - s0]
-            return got
-
-        def gather_bytes(half, tag):
-            got = keep.tile([P, HALF], U8, name="got_bytes_%d" % half, tag=tag, align_bytes=64)
-            nc.vector.tensor_copy(out=got[:], in_=all_bytes[:].indirect(entries(half)))
-            got_bytes[half] = got
-
-        for z in range(PASSES):
+        def round_and_gather(pair):
+            z, u = divmod(pair, 2)
+            pairs = keep.tile([P, T, 2], BF16, name="pairs_%d" % pair, align_bytes=64)
             c0 = 0
-            for i, width in enumerate(X_CHUNKS[z]):
-                raw = x_raw[z, i]
-                for a in range(0, width, 512):
-                    piece = min(width - a, 512)
-                    xb = keep.tile([P, piece, PACK], BF16, name="x_bf_%d_%d_%d" % (z, i, a), align_bytes=64)
-                    cut = piece * X_CUT[z][i] // 8
-                    nc.scalar.activation(
-                        out=xb[:, 0:cut, :].rearrange("p (c i) j -> p c j i", i=4),
-                        in_=raw[:, :, a:a + cut].rearrange("p j (c i) -> p c j i", i=4), func=COPY)
-                    if cut < piece:
-                        nc.vector.tensor_copy(
-                            out=xb[:, cut:piece, :].rearrange("p (c i) j -> p c j i", i=4),
-                            in_=raw[:, :, a + cut:a + piece].rearrange("p j (c i) -> p c j i", i=4))
-                    nc.vector.quantize_mx(
-                        out=all_words[z][:, c0 + a:c0 + a + piece].bitcast(FP8X4),
-                        scales=all_bytes[4 * z:P, c0 + a:c0 + a + piece],
-                        in_=xb[:].rearrange("p c j -> p (c j)"))
+            for i, (width, cut) in enumerate(X_LOADS[pair]):
+                src = x_raw[pair, i][:].rearrange("p e c -> p c e")
+                if cut > 0:
+                    nc.scalar.activation(out=pairs[:, c0:c0 + cut, :], in_=src[:, 0:cut, :], func=COPY)
+                if cut < width:
+                    nc.vector.tensor_copy(out=pairs[:, c0 + cut:c0 + width, :], in_=src[:, cut:width, :])
                 c0 = c0 + width
-            if z == 0:
-                gather_words(0, 0, HALF, "got_words_0_0")
-                early = gather_words(0, HALF, HALF, "got_words_0_1")
+            window = pairs[:].rearrange("p c e -> p (c e)").bitcast(U32)
+            for half in range(2):
+                if u == 0:
+                    got[z, half] = keep.tile([P, 2, HALF], U32, name="got_%d_%d" % (z, half), align_bytes=64)
+                nc.vector.tensor_copy(out=got[z, half][:, u, :],
+                                      in_=window.indirect(offsets[:, half * (HALF // 16):(half + 1) * (HALF // 16)]))
+
+        def weave(z, half):
+            if (z, half) == (1, 1):
+                tile = held.tile([P, HALF, 2], I32, name="woven_last", offset=512, align_bytes=64)
+            else:
+                tile = keep.tile([P, HALF, 2], I32, name="woven_%d_%d" % (z, half), align_bytes=64)
+            nc.vector.tensor_copy(out=tile[:], in_=got[z, half][:].bitcast(I32).rearrange("p u c -> p c u"))
+            woven[z, half] = tile
+
+        def quantise_x(z, half):
+            if z == 1:
+                codes = held.tile([P, HALF], U32, name="x_codes_1_%d" % half, offset=(4608, 8192)[half], align_bytes=64)
+            else:
+                codes = keep.tile([P, HALF], U32, name="x_codes_0_%d" % half, align_bytes=64)
+            scales = keep.tile([P, HALF], U8, name="x_bytes_%d_%d" % (z, half), align_bytes=64)
+            nc.vector.quantize_mx(out=codes[:].bitcast(FP8X4), scales=scales[:],
+                                  in_=woven[z, half][:].rearrange("p c u -> p (c u)").bitcast(BF16))
+            x_codes[z, half] = codes
+            x_bytes[z, half] = scales
+
+        round_and_gather(0)
+        round_and_gather(1)
+        weave(0, 0)
+        weave(0, 1)
+        quantise_x(0, 0)
+        quantise_x(0, 1)
+        round_and_gather(2)
+        round_and_gather(3)
+        weave(1, 0)
 
         w_codes = []
         w_bytes = []
@@ -130,7 +149,10 @@ def tile_picked_embpos_gelu_e_kernel(tc, xT, w1, w2_words, w2_scales, pos, offs,
             m0 = 0
             for i, width in enumerate(W_CHUNKS[z]):
                 src = w_raw[z, i][:].rearrange("p j (m t) -> p m j t", t=PACK)
-                nc.scalar.activation(out=dst[:, m0:m0 + width // PACK], in_=src, func=COPY)
+                cut = width // PACK - (W_SHARE if (z, i) == (0, 1) else 0)
+                nc.scalar.activation(out=dst[:, m0:m0 + cut], in_=src[:, 0:cut], func=COPY)
+                if cut < width // PACK:
+                    nc.vector.tensor_copy(out=dst[:, m0 + cut:m0 + width // PACK], in_=src[:, cut:width // PACK])
                 m0 = m0 + width // PACK
             codes = keep.tile([P, H], U32, name="w_codes_%d" % z, align_bytes=64)
             scales = keep.tile([P, H], U8, name="w_bytes_%d" % z, align_bytes=64)
@@ -152,37 +174,23 @@ def tile_picked_embpos_gelu_e_kernel(tc, xT, w1, w2_words, w2_scales, pos, offs,
                 out=acc[g][:, t, :],
                 lhsT=w_codes[z][:, t * P:(t + 1) * P].bitcast(FP8X4),
                 lhsT_scale=w_bytes[z][:, t * P:(t + 1) * P],
-                rhs=got_words[z, g].bitcast(FP8X4),
-                rhs_scale=got_bytes[half][4 * z:P, a:a + GROUP],
-                start=(z == 0), stop=(z == PASSES - 1))
+                rhs=x_codes[z, half][:, a:a + GROUP].bitcast(FP8X4),
+                rhs_scale=x_bytes[z, half][:, a:a + GROUP],
+                start=(z == 0 and t == 0), stop=(z == PASSES - 1 and t == PACK - 1))
 
-        gather_bytes(0, "got_bytes_0")
-        gather_bytes(1, "got_bytes_1")
-        idle = psum.tile([P, HALF], F32, name="idle", tag="bank_7")
+        def product(g, z):
+            for t in range(PACK):
+                product_pass(g, t, z)
 
-        def warm_up(stationary):
-            nc.tensor.matmul_mx(out=idle[:], lhsT=stationary.bitcast(FP8X4), lhsT_scale=got_bytes[0][:, 0:P],
-                                rhs=early[:].bitcast(FP8X4), rhs_scale=got_bytes[1][:], start=True, stop=True)
-
-        warm_up(got_words[0, 0])
-        warm_up(got_words[0, 0])
-        gather_words(1, 0, 512, "got_words_1_0")
-        warm_up(got_words[1, 0])
-        gather_words(1, 512, 256, "got_words_1_1")
-        warm_up(got_words[1, 4])
         quantise_w1(0)
         for g in range(RING):
-            product_pass(g, 0, 0)
+            product(g, 0)
+        weave(1, 1)
+        quantise_x(1, 0)
         quantise_w1(1)
-        gather_words(1, 768, 256, "w_bf_1")
-
-        def finish_first_product(g):
-            if g >= RING:
-                product_pass(g, 0, 0)
-            product_pass(g, 0, 1)
-            for t in range(1, PACK):
-                for z in range(PASSES):
-                    product_pass(g, t, z)
+        quantise_x(1, 1)
+        for g in range(RING):
+            product(g, 1)
 
         hidden = {}
         h_tiles = []
@@ -220,14 +228,13 @@ def tile_picked_embpos_gelu_e_kernel(tc, xT, w1, w2_words, w2_scales, pos, offs,
             queue = nc.scalar if r == len(RUNS) - 1 else nc.sync
             queue.dma_start(out=out[:, s0:s0 + n], in_=res[:])
 
-        for g in range(RING):
-            finish_first_product(g)
         for g in range(groups):
             for r, run in enumerate(RUNS):
                 if g in run:
                     add_pos_and_gelu(r, run.index(g))
             if g + RING < groups:
-                finish_first_product(g + RING)
+                product(g + RING, 0)
+                product(g + RING, 1)
             if g == 5:
                 second_product(0)
         for r in range(1, len(RUNS)):

@@ -27,7 +27,8 @@ X_LOADS = (
     ((512, 512), (512, 512), (512, 512), (512, 512)),
     ((768, 768), (768, 512), (256, 0), (256, 128)),
 )
-W_SHARE = 0
+W_SHARE = 32
+PIECES = (((0, 512), (512, 512)), ((0, 256), (256, 256), (512, 512)))
 W_CHUNKS = ((256, 256), (256, 128, 128))
 POS_CHUNKS = (256, 256, 256, 256)
 W_CALLS = (1, 2)
@@ -62,10 +63,8 @@ def tile_picked_embpos_gelu_e_kernel(tc, xT, w1, w2_words, w2_scales, pos, offs,
             rows = w1[z * K_PASS:(z + 1) * K_PASS, :].rearrange("(p j) c -> p j c", j=PACK)
             c0 = 0
             for i, width in enumerate(W_CHUNKS[z]):
-                if (z, i) == (0, 1):
-                    raw = held.tile([P, PACK, width], F32, name="w_raw_0_last", offset=4096, align_bytes=64)
-                elif (z, i) == (1, 2):
-                    raw = held.tile([P, PACK, width], F32, name="w_raw_1_last", offset=8192, align_bytes=64)
+                if (z, i) == (1, 2):
+                    raw = held.tile([P, PACK, width], F32, name="w_raw_1_last", offset=0, align_bytes=64)
                 else:
                     raw = keep.tile([P, PACK, width], F32, name="w_raw_%d_%d" % (z, i))
                 nc.sync.dma_start(out=raw[:], in_=rows[:, :, c0:c0 + width])
@@ -93,8 +92,9 @@ def tile_picked_embpos_gelu_e_kernel(tc, xT, w1, w2_words, w2_scales, pos, offs,
         x_codes = {}
         x_bytes = {}
 
-        def round_and_gather(pair):
-            z, u = divmod(pair, 2)
+        windows = {}
+
+        def round_pair(pair):
             pairs = keep.tile([P, T, 2], BF16, name="pairs_%d" % pair, align_bytes=64)
             c0 = 0
             for i, (width, cut) in enumerate(X_LOADS[pair]):
@@ -104,41 +104,62 @@ def tile_picked_embpos_gelu_e_kernel(tc, xT, w1, w2_words, w2_scales, pos, offs,
                 if cut < width:
                     nc.vector.tensor_copy(out=pairs[:, c0 + cut:c0 + width, :], in_=src[:, cut:width, :])
                 c0 = c0 + width
-            window = pairs[:].rearrange("p c e -> p (c e)").bitcast(U32)
-            for half in range(2):
-                if u == 0:
-                    got[z, half] = keep.tile([P, 2, HALF], U32, name="got_%d_%d" % (z, half), align_bytes=64)
-                nc.vector.tensor_copy(out=got[z, half][:, u, :],
-                                      in_=window.indirect(offsets[:, half * (HALF // 16):(half + 1) * (HALF // 16)]))
+            windows[pair] = pairs[:].rearrange("p c e -> p (c e)").bitcast(U32)
 
-        def weave(z, half):
-            if (z, half) == (1, 1):
-                tile = held.tile([P, HALF, 2], I32, name="woven_last", offset=512, align_bytes=64)
-            else:
-                tile = keep.tile([P, HALF, 2], I32, name="woven_%d_%d" % (z, half), align_bytes=64)
-            nc.vector.tensor_copy(out=tile[:], in_=got[z, half][:].bitcast(I32).rearrange("p u c -> p c u"))
-            woven[z, half] = tile
+        def gather(z, u, i):
+            s0, n = PIECES[z][i]
+            if u == 0:
+                got[z, i] = keep.tile([P, 2, n], U32, name="got_%d_%d" % (z, i), align_bytes=64)
+            nc.vector.tensor_copy(out=got[z, i][:, u, :], in_=windows[2 * z + u].indirect(offsets[:, s0 // 16:(s0 + n) // 16]))
 
-        def quantise_x(z, half):
-            if z == 1:
-                codes = held.tile([P, HALF], U32, name="x_codes_1_%d" % half, offset=(4608, 8192)[half], align_bytes=64)
+        def weave(z, i):
+            n = PIECES[z][i][1]
+            tile = keep.tile([P, n, 2], I32, name="woven_%d_%d" % (z, i), align_bytes=64)
+            nc.vector.tensor_copy(out=tile[:], in_=got[z, i][:].bitcast(I32).rearrange("p u c -> p c u"))
+            woven[z, i] = tile
+
+        def quantise_x(z, i):
+            s0, n = PIECES[z][i]
+            if (z, i) == (1, 2):
+                codes = held.tile([P, n], U32, name="x_codes_last", offset=0, align_bytes=64)
             else:
-                codes = keep.tile([P, HALF], U32, name="x_codes_0_%d" % half, align_bytes=64)
-            scales = keep.tile([P, HALF], U8, name="x_bytes_%d_%d" % (z, half), align_bytes=64)
+                codes = keep.tile([P, n], U32, name="x_codes_%d_%d" % (z, i), align_bytes=64)
+            scales = keep.tile([P, n], U8, name="x_bytes_%d_%d" % (z, i), align_bytes=64)
             nc.vector.quantize_mx(out=codes[:].bitcast(FP8X4), scales=scales[:],
-                                  in_=woven[z, half][:].rearrange("p c u -> p (c u)").bitcast(BF16))
-            x_codes[z, half] = codes
-            x_bytes[z, half] = scales
+                                  in_=woven[z, i][:].rearrange("p c u -> p (c u)").bitcast(BF16))
+            for a in range(0, n, GROUP):
+                x_codes[z, (s0 + a) // GROUP] = codes[:, a:a + GROUP]
+                x_bytes[z, (s0 + a) // GROUP] = scales[:, a:a + GROUP]
+            return codes, scales
 
-        round_and_gather(0)
-        round_and_gather(1)
+        for u in range(2):
+            round_pair(u)
+            for i in range(2):
+                gather(0, u, i)
         weave(0, 0)
         weave(0, 1)
-        quantise_x(0, 0)
+        early_codes, early_bytes = quantise_x(0, 0)
         quantise_x(0, 1)
-        round_and_gather(2)
-        round_and_gather(3)
+        round_pair(2)
+        for i in range(3):
+            gather(1, 0, i)
+        round_pair(3)
+        idle = psum.tile([P, HALF], F32, name="idle", tag="bank_7")
+
+        def warm_up(g):
+            nc.tensor.matmul_mx(out=idle[:], lhsT=x_codes[1, g].bitcast(FP8X4), lhsT_scale=x_bytes[1, g],
+                                rhs=early_codes[:].bitcast(FP8X4), rhs_scale=early_bytes[:], start=True, stop=True)
+
+        gather(1, 1, 0)
+        gather(1, 1, 1)
         weave(1, 0)
+        gather(1, 1, 2)
+        quantise_x(1, 0)
+        for repeat in range(3):
+            warm_up(0)
+        weave(1, 1)
+        weave(1, 2)
+        quantise_x(1, 1)
 
         w_codes = []
         w_bytes = []
@@ -149,7 +170,7 @@ def tile_picked_embpos_gelu_e_kernel(tc, xT, w1, w2_words, w2_scales, pos, offs,
             m0 = 0
             for i, width in enumerate(W_CHUNKS[z]):
                 src = w_raw[z, i][:].rearrange("p j (m t) -> p m j t", t=PACK)
-                cut = width // PACK - (W_SHARE if (z, i) == (0, 1) else 0)
+                cut = width // PACK - (W_SHARE if (z, i) == (1, 0) else 0)
                 nc.scalar.activation(out=dst[:, m0:m0 + cut], in_=src[:, 0:cut], func=COPY)
                 if cut < width // PACK:
                     nc.vector.tensor_copy(out=dst[:, m0 + cut:m0 + width // PACK], in_=src[:, cut:width // PACK])
@@ -167,30 +188,31 @@ def tile_picked_embpos_gelu_e_kernel(tc, xT, w1, w2_words, w2_scales, pos, offs,
         acc = {}
 
         def product_pass(g, t, z):
-            half, a = divmod(g * GROUP, HALF)
             if t == 0 and z == 0:
                 acc[g] = psum.tile([P, PACK, GROUP], F32, name="acc_%d" % g, tag="bank_%d" % (g % RING))
             nc.tensor.matmul_mx(
                 out=acc[g][:, t, :],
                 lhsT=w_codes[z][:, t * P:(t + 1) * P].bitcast(FP8X4),
                 lhsT_scale=w_bytes[z][:, t * P:(t + 1) * P],
-                rhs=x_codes[z, half][:, a:a + GROUP].bitcast(FP8X4),
-                rhs_scale=x_bytes[z, half][:, a:a + GROUP],
-                start=(z == 0 and t == 0), stop=(z == PASSES - 1 and t == PACK - 1))
+                rhs=x_codes[z, g].bitcast(FP8X4),
+                rhs_scale=x_bytes[z, g],
+                start=(z == 0), stop=(z == PASSES - 1))
 
-        def product(g, z):
-            for t in range(PACK):
-                product_pass(g, t, z)
+        def finish_first_product(g):
+            if g >= RING:
+                product_pass(g, 0, 0)
+            product_pass(g, 0, 1)
+            for t in range(1, PACK):
+                for z in range(PASSES):
+                    product_pass(g, t, z)
 
         quantise_w1(0)
         for g in range(RING):
-            product(g, 0)
-        weave(1, 1)
-        quantise_x(1, 0)
+            product_pass(g, 0, 0)
         quantise_w1(1)
-        quantise_x(1, 1)
+        quantise_x(1, 2)
         for g in range(RING):
-            product(g, 1)
+            finish_first_product(g)
 
         hidden = {}
         h_tiles = []
@@ -233,8 +255,7 @@ def tile_picked_embpos_gelu_e_kernel(tc, xT, w1, w2_words, w2_scales, pos, offs,
                 if g in run:
                     add_pos_and_gelu(r, run.index(g))
             if g + RING < groups:
-                product(g + RING, 0)
-                product(g + RING, 1)
+                finish_first_product(g + RING)
             if g == 5:
                 second_product(0)
         for r in range(1, len(RUNS)):

@@ -20,171 +20,184 @@ P = 128
 PACK = 4
 K_PASS = P * PACK
 PASSES = K // K_PASS
-HALF = 512
+HALF = S // 2
+STRIPE = 16
+QUADRANT = 32
+BANKS = 8
+
 X_LOADS = (
     ((2048, 704),),
     ((1024, 1024), (768, 0), (256, 256)),
     ((512, 512), (512, 512), (512, 512), (512, 512)),
     ((768, 768), (768, 512), (256, 0), (256, 128)),
 )
-W_SHARE = 32
 PIECES = (((0, 512), (512, 512)), ((0, 256), (256, 256), (512, 512)))
-W_CHUNKS = ((256, 256), (256, 128, 128))
-POS_CHUNKS = (256, 256, 256, 256)
+LAST_PIECE = len(PIECES[1]) - 1
+W_LOADS = (((256, 256), (256, 256)), ((256, 128), (128, 128), (128, 128)))
 W_CALLS = (1, 2)
+POS_LOAD = 256
 GROUP = 128
+GROUPS = S // GROUP
 RING = 4
 RUNS = ((0, 1), (2, 3), (4, 5), (6,), (7,))
+VECTOR_RUN = 2
+EARLY_WARM_UPS = 3
 
 
 def tile_picked_embpos_gelu_e_kernel(tc, xT, w1, w2_words, w2_scales, pos, offs, out):
     nc = tc.nc
     with ExitStack() as ctx:
         keep = ctx.enter_context(tc.tile_pool(name="keep", bufs=1))
-        held = ctx.enter_context(tc.tile_pool(name="held", bufs=1))
+        reused = ctx.enter_context(tc.tile_pool(name="reused", bufs=1))
         psum = ctx.enter_context(tc.psum_pool(name="psum", bufs=1))
 
-        offsets = keep.tile([P, S // 16], U16, name="offsets")
+        offsets = keep.tile([P, S // STRIPE], U16, name="offsets")
 
         x_raw = {}
         for pair, loads in enumerate(X_LOADS):
             z, u = divmod(pair, 2)
             rows = xT[z * K_PASS:(z + 1) * K_PASS, :].rearrange("(p j) c -> p j c", j=PACK)
             c0 = 0
-            for i, (width, cut) in enumerate(loads):
+            for i, (width, scalar_cols) in enumerate(loads):
                 raw = keep.tile([P, 2, width], F32, name="x_raw_%d_%d" % (pair, i))
                 nc.sync.dma_start(out=raw[:], in_=rows[:, 2 * u:2 * u + 2, c0:c0 + width])
                 x_raw[pair, i] = raw
                 c0 = c0 + width
             if pair == 0:
                 nc.sync.dma_start(offsets[:], offs)
+
         w_raw = {}
         for z in range(PASSES):
             rows = w1[z * K_PASS:(z + 1) * K_PASS, :].rearrange("(p j) c -> p j c", j=PACK)
             c0 = 0
-            for i, width in enumerate(W_CHUNKS[z]):
-                if (z, i) == (1, 2):
-                    raw = held.tile([P, PACK, width], F32, name="w_raw_1_last", offset=0, align_bytes=64)
+            for i, (width, scalar_cols) in enumerate(W_LOADS[z]):
+                if z == PASSES - 1 and i == len(W_LOADS[z]) - 1:
+                    raw = reused.tile([P, PACK, width], F32, name="w_raw_last", offset=0, align_bytes=64)
                 else:
                     raw = keep.tile([P, PACK, width], F32, name="w_raw_%d_%d" % (z, i))
                 nc.sync.dma_start(out=raw[:], in_=rows[:, :, c0:c0 + width])
                 w_raw[z, i] = raw
                 c0 = c0 + width
+
         w2_codes = keep.tile([P, N], U32, name="w2_codes", align_bytes=64)
         w2_bytes = keep.tile([P, N], U8, name="w2_bytes", align_bytes=64)
         nc.vector.memset(w2_bytes[:].bitcast(I32), 0)
-        for q in range(4):
-            nc.sync.dma_start(out=w2_bytes[32 * q:32 * q + 4, :].bitcast(I32), in_=w2_scales[0, 4 * q:4 * q + 4, :].bitcast(I32))
+        for q in range(P // QUADRANT):
+            nc.sync.dma_start(out=w2_bytes[QUADRANT * q:QUADRANT * q + 4, :].bitcast(I32),
+                              in_=w2_scales[0, 4 * q:4 * q + 4, :].bitcast(I32))
         nc.sync.dma_start(out=w2_codes[:].bitcast(I32), in_=w2_words[0].rearrange("p n r -> p (n r)").bitcast(I32))
 
         pos_rows = pos.rearrange("(p t) s -> p t s", t=PACK)
-        pos_sb = []
-        s0 = 0
-        for width in POS_CHUNKS:
-            raw = keep.tile([P, PACK, width], F32, name="pos_%d" % s0, tag="pos_%d" % s0, align_bytes=64)
-            nc.sync.dma_start(out=raw[:], in_=pos_rows[:, :, s0:s0 + width])
-            for a in range(0, width, GROUP):
-                pos_sb.append(raw[:, :, a:a + GROUP])
-            s0 = s0 + width
+        pos_of_group = []
+        for s0 in range(0, S, POS_LOAD):
+            raw = keep.tile([P, PACK, POS_LOAD], F32, name="pos_%d" % s0, tag="pos_%d" % s0, align_bytes=64)
+            nc.sync.dma_start(out=raw[:], in_=pos_rows[:, :, s0:s0 + POS_LOAD])
+            for a in range(0, POS_LOAD, GROUP):
+                pos_of_group.append(raw[:, :, a:a + GROUP])
 
-        got = {}
+        windows = {}
+        gathered = {}
         woven = {}
         x_codes = {}
         x_bytes = {}
 
-        windows = {}
-
-        def round_pair(pair):
+        def round_pair(z, u):
+            pair = 2 * z + u
             pairs = keep.tile([P, T, 2], BF16, name="pairs_%d" % pair, align_bytes=64)
             c0 = 0
-            for i, (width, cut) in enumerate(X_LOADS[pair]):
+            for i, (width, scalar_cols) in enumerate(X_LOADS[pair]):
                 src = x_raw[pair, i][:].rearrange("p e c -> p c e")
-                if cut > 0:
-                    nc.scalar.activation(out=pairs[:, c0:c0 + cut, :], in_=src[:, 0:cut, :], func=COPY)
-                if cut < width:
-                    nc.vector.tensor_copy(out=pairs[:, c0 + cut:c0 + width, :], in_=src[:, cut:width, :])
+                if scalar_cols > 0:
+                    nc.scalar.activation(out=pairs[:, c0:c0 + scalar_cols, :], in_=src[:, 0:scalar_cols, :], func=COPY)
+                if scalar_cols < width:
+                    nc.vector.tensor_copy(out=pairs[:, c0 + scalar_cols:c0 + width, :], in_=src[:, scalar_cols:width, :])
                 c0 = c0 + width
-            windows[pair] = pairs[:].rearrange("p c e -> p (c e)").bitcast(U32)
+            windows[z, u] = pairs[:].rearrange("p c e -> p (c e)").bitcast(U32)
 
-        def gather(z, u, i):
-            s0, n = PIECES[z][i]
-            if u == 0:
-                got[z, i] = keep.tile([P, 2, n], U32, name="got_%d_%d" % (z, i), align_bytes=64)
-            nc.vector.tensor_copy(out=got[z, i][:, u, :], in_=windows[2 * z + u].indirect(offsets[:, s0 // 16:(s0 + n) // 16]))
+        def gather(z, u, piece):
+            s0, n = PIECES[z][piece]
+            if (z, piece) not in gathered:
+                gathered[z, piece] = keep.tile([P, 2, n], U32, name="gathered_%d_%d" % (z, piece), align_bytes=64)[:]
+            nc.vector.tensor_copy(out=gathered[z, piece][:, u, :],
+                                  in_=windows[z, u].indirect(offsets[:, s0 // STRIPE:(s0 + n) // STRIPE]))
 
-        def weave(z, i):
-            n = PIECES[z][i][1]
-            tile = keep.tile([P, n, 2], I32, name="woven_%d_%d" % (z, i), align_bytes=64)
-            nc.vector.tensor_copy(out=tile[:], in_=got[z, i][:].bitcast(I32).rearrange("p u c -> p c u"))
-            woven[z, i] = tile
+        def weave(z, piece):
+            n = PIECES[z][piece][1]
+            woven[z, piece] = keep.tile([P, n, 2], I32, name="woven_%d_%d" % (z, piece), align_bytes=64)
+            nc.vector.tensor_copy(out=woven[z, piece][:], in_=gathered[z, piece].bitcast(I32).rearrange("p u c -> p c u"))
 
-        def quantise_x(z, i):
-            s0, n = PIECES[z][i]
-            if (z, i) == (1, 2):
-                codes = held.tile([P, n], U32, name="x_codes_last", offset=0, align_bytes=64)
+        def quantise_x(z, piece):
+            s0, n = PIECES[z][piece]
+            if (z, piece) == (1, LAST_PIECE):
+                codes = reused.tile([P, n], U32, name="x_codes_last", offset=0, align_bytes=64)
             else:
-                codes = keep.tile([P, n], U32, name="x_codes_%d_%d" % (z, i), align_bytes=64)
-            scales = keep.tile([P, n], U8, name="x_bytes_%d_%d" % (z, i), align_bytes=64)
+                codes = keep.tile([P, n], U32, name="x_codes_%d_%d" % (z, piece), align_bytes=64)
+            scales = keep.tile([P, n], U8, name="x_bytes_%d_%d" % (z, piece), align_bytes=64)
             nc.vector.quantize_mx(out=codes[:].bitcast(FP8X4), scales=scales[:],
-                                  in_=woven[z, i][:].rearrange("p c u -> p (c u)").bitcast(BF16))
+                                  in_=woven[z, piece][:].rearrange("p c u -> p (c u)").bitcast(BF16))
             for a in range(0, n, GROUP):
                 x_codes[z, (s0 + a) // GROUP] = codes[:, a:a + GROUP]
                 x_bytes[z, (s0 + a) // GROUP] = scales[:, a:a + GROUP]
             return codes, scales
 
         for u in range(2):
-            round_pair(u)
-            for i in range(2):
-                gather(0, u, i)
+            round_pair(0, u)
+            for piece in range(len(PIECES[0])):
+                gather(0, u, piece)
         weave(0, 0)
         weave(0, 1)
-        early_codes, early_bytes = quantise_x(0, 0)
+        first_codes, first_bytes = quantise_x(0, 0)
         quantise_x(0, 1)
-        round_pair(2)
-        for i in range(3):
-            gather(1, 0, i)
-        round_pair(3)
-        idle = psum.tile([P, HALF], F32, name="idle", tag="bank_7")
+
+        shared = keep.tile([P, 2 * HALF], U32, name="gathered_shared", align_bytes=64)
+        gathered[1, LAST_PIECE] = shared[:].rearrange("p (u c) -> p u c", u=2)
+        gathered[1, 0] = shared[:, HALF:2 * HALF].rearrange("p (u c) -> p u c", u=2)
+        round_pair(1, 0)
+        for piece in range(len(PIECES[1])):
+            gather(1, 0, piece)
+        round_pair(1, 1)
+
+        unread = psum.tile([P, HALF], F32, name="unread", tag="bank_%d" % (BANKS - 1))
 
         def warm_up(g):
-            nc.tensor.matmul_mx(out=idle[:], lhsT=x_codes[1, g].bitcast(FP8X4), lhsT_scale=x_bytes[1, g],
-                                rhs=early_codes[:].bitcast(FP8X4), rhs_scale=early_bytes[:], start=True, stop=True)
+            nc.tensor.matmul_mx(out=unread[:], lhsT=x_codes[1, g].bitcast(FP8X4), lhsT_scale=x_bytes[1, g],
+                                rhs=first_codes[:].bitcast(FP8X4), rhs_scale=first_bytes[:], start=True, stop=True)
 
         gather(1, 1, 0)
         gather(1, 1, 1)
         weave(1, 0)
-        gather(1, 1, 2)
-        quantise_x(1, 0)
-        for repeat in range(3):
-            warm_up(0)
         weave(1, 1)
-        weave(1, 2)
+        quantise_x(1, 0)
+        for repeat in range(EARLY_WARM_UPS):
+            warm_up(0)
+        gather(1, 1, LAST_PIECE)
         quantise_x(1, 1)
+        warm_up(PIECES[1][1][0] // GROUP)
+        weave(1, LAST_PIECE)
 
         w_codes = []
         w_bytes = []
 
         def quantise_w1(z):
-            wb = keep.tile([P, PACK, P, PACK], BF16, name="w_bf_%d" % z, tag="w_bf_%d" % z, align_bytes=64)
-            dst = wb[:].rearrange("p t m j -> p m j t")
+            rounded = keep.tile([P, PACK, P, PACK], BF16, name="w_rounded_%d" % z, align_bytes=64)
+            dst = rounded[:].rearrange("p t m j -> p m j t")
             m0 = 0
-            for i, width in enumerate(W_CHUNKS[z]):
+            for i, (width, scalar_cols) in enumerate(W_LOADS[z]):
                 src = w_raw[z, i][:].rearrange("p j (m t) -> p m j t", t=PACK)
-                cut = width // PACK - (W_SHARE if (z, i) == (1, 0) else 0)
-                nc.scalar.activation(out=dst[:, m0:m0 + cut], in_=src[:, 0:cut], func=COPY)
-                if cut < width // PACK:
-                    nc.vector.tensor_copy(out=dst[:, m0 + cut:m0 + width // PACK], in_=src[:, cut:width // PACK])
-                m0 = m0 + width // PACK
+                m_all, m_scalar = width // PACK, scalar_cols // PACK
+                nc.scalar.activation(out=dst[:, m0:m0 + m_scalar], in_=src[:, 0:m_scalar], func=COPY)
+                if m_scalar < m_all:
+                    nc.vector.tensor_copy(out=dst[:, m0 + m_scalar:m0 + m_all], in_=src[:, m_scalar:m_all])
+                m0 = m0 + m_all
             codes = keep.tile([P, H], U32, name="w_codes_%d" % z, align_bytes=64)
             scales = keep.tile([P, H], U8, name="w_bytes_%d" % z, align_bytes=64)
             step = H // W_CALLS[z]
             for c in range(0, H, step):
                 nc.vector.quantize_mx(out=codes[:, c:c + step].bitcast(FP8X4), scales=scales[:, c:c + step],
-                                      in_=wb[:].rearrange("p t m j -> p (t m j)")[:, PACK * c:PACK * (c + step)])
+                                      in_=rounded[:].rearrange("p t m j -> p (t m j)")[:, PACK * c:PACK * (c + step)])
             w_codes.append(codes)
             w_bytes.append(scales)
 
-        groups = S // GROUP
         acc = {}
 
         def product_pass(g, t, z):
@@ -210,53 +223,54 @@ def tile_picked_embpos_gelu_e_kernel(tc, xT, w1, w2_words, w2_scales, pos, offs,
         for g in range(RING):
             product_pass(g, 0, 0)
         quantise_w1(1)
-        quantise_x(1, 2)
+        quantise_x(1, LAST_PIECE)
         for g in range(RING):
             finish_first_product(g)
 
         hidden = {}
-        h_tiles = []
+        h_code_tiles = {}
 
         def add_pos_and_gelu(r, i):
             g = RUNS[r][i]
             pre = keep.tile([P, PACK, GROUP], F32, name="pre_%d" % g)
-            nc.vector.tensor_tensor(out=pre[:], in0=acc[g][:], in1=pos_sb[g], op=ADD)
+            nc.vector.tensor_tensor(out=pre[:], in0=acc[g][:], in1=pos_of_group[g], op=ADD)
             if i == 0:
-                hidden[r] = keep.tile([P, GROUP * len(RUNS[r]), PACK], BF16, name="hidden_%d" % r, tag="hidden_%d" % r, align_bytes=64)
+                hidden[r] = keep.tile([P, GROUP * len(RUNS[r]), PACK], BF16, name="hidden_%d" % r, align_bytes=64)
             nc.scalar.activation(
-                out=hidden[r][:, i * GROUP:(i + 1) * GROUP, :].rearrange("p (c i) t -> p c t i", i=4),
-                in_=pre[:].rearrange("p t (c i) -> p c t i", i=4), func=GELU)
+                out=hidden[r][:, i * GROUP:(i + 1) * GROUP, :].rearrange("p (c e) t -> p c t e", e=4),
+                in_=pre[:].rearrange("p t (c e) -> p c t e", e=4), func=GELU)
 
         def second_product(r):
             s0 = RUNS[r][0] * GROUP
             n = GROUP * len(RUNS[r])
             if r == 0:
-                h_tiles.append(keep.tile([P, n], U32, name="h_codes_first", tag="pos_512", align_bytes=64))
-                h_codes = h_tiles[0][:]
+                h_code_tiles["first"] = keep.tile([P, n], U32, name="h_codes_first", tag="pos_%d" % (S - 2 * POS_LOAD), align_bytes=64)
+                h_codes = h_code_tiles["first"][:]
             else:
                 if r == 1:
-                    h_tiles.append(keep.tile([P, S], U32, name="h_codes_rest", tag="pos_768", align_bytes=64))
-                h_codes = h_tiles[1][:, s0:s0 + n]
+                    h_code_tiles["rest"] = keep.tile([P, S], U32, name="h_codes_rest", tag="pos_%d" % (S - POS_LOAD), align_bytes=64)
+                h_codes = h_code_tiles["rest"][:, s0:s0 + n]
             h_bytes = keep.tile([P, n], U8, name="h_bytes_%d" % r, align_bytes=64)
             nc.vector.quantize_mx(out=h_codes.bitcast(FP8X4), scales=h_bytes[:], in_=hidden[r][:].rearrange("p c t -> p (c t)"))
-            sums = psum.tile([P, n], F32, name="sums_%d" % r, tag="bank_%d" % (RING + r % (8 - RING)))
+            sums = psum.tile([P, n], F32, name="sums_%d" % r, tag="bank_%d" % (RING + r % (BANKS - RING)))
             nc.tensor.matmul_mx(out=sums[:], lhsT=w2_codes[:].bitcast(FP8X4), lhsT_scale=w2_bytes[:],
                                 rhs=h_codes.bitcast(FP8X4), rhs_scale=h_bytes[:], start=True, stop=True)
-            res = keep.tile([P, n], F32, name="res_%d" % r)
-            if r == 2:
-                nc.vector.tensor_copy(out=res[:], in_=sums[:])
+            result = keep.tile([P, n], F32, name="result_%d" % r)
+            if r == VECTOR_RUN:
+                nc.vector.tensor_copy(out=result[:], in_=sums[:])
             else:
-                nc.scalar.activation(out=res[:], in_=sums[:], func=COPY)
+                nc.scalar.activation(out=result[:], in_=sums[:], func=COPY)
             queue = nc.scalar if r == len(RUNS) - 1 else nc.sync
-            queue.dma_start(out=out[:, s0:s0 + n], in_=res[:])
+            queue.dma_start(out=out[:, s0:s0 + n], in_=result[:])
 
-        for g in range(groups):
+        last_group_of_third_load = (S - POS_LOAD) // GROUP - 1
+        for g in range(GROUPS):
             for r, run in enumerate(RUNS):
                 if g in run:
                     add_pos_and_gelu(r, run.index(g))
-            if g + RING < groups:
+            if g + RING < GROUPS:
                 finish_first_product(g + RING)
-            if g == 5:
+            if g == last_group_of_third_load:
                 second_product(0)
         for r in range(1, len(RUNS)):
             second_product(r)

@@ -31,24 +31,33 @@ X_LOADS = (
     ((512, 512), (512, 512), (512, 512), (512, 512)),
     ((768, 768), (768, 512), (256, 0), (256, 128)),
 )
-PIECES = (((0, 512), (512, 512)), ((0, 256), (256, 256), (512, 512)))
-LAST_PIECE = len(PIECES[1]) - 1
-W_LOADS = (((256, 256), (256, 256)), ((256, 128), (128, 128), (128, 128)))
-W_CALLS = (1, 2)
-POS_LOAD = 256
+PIECES = (((0, 512), (512, 256), (768, 128), (896, 128)), ((0, 512), (512, 512)))
+HOLD_X_LOAD = (3, 3)
+LAST_GATHERS = (256, 256, 512)
+W_LOADS = (((256, 256), (256, 256)), ((256, 256), (128, 0), (128, 128)))
+W_SPLIT = ((2, 1), (2, 1))
+POS_LOADS = (256, 256, 256, 256)
 GROUP = 128
 GROUPS = S // GROUP
 RING = 4
-RUNS = ((0, 1), (2, 3), (4, 5), (6,), (7,))
-VECTOR_RUN = 2
-EARLY_WARM_UPS = 3
+STEPS = (32, 96, 128, 128, 128, 128, 128, 128, 64, 64)
+H_CALLS = (256, 256, 256, 128, 64, 64)
+RUNS = (256, 256, 256, 128, 128)
+RUN_BANKS = (4, 5, 6, 7, 4)
+VECTOR_RUNS = (2,)
+EARLY_CALLS = 0
+HOLD_STEP = 640
+WARM_UPS = 4
+
+
+def starts(widths):
+    return [sum(widths[:i]) for i in range(len(widths))]
 
 
 def tile_picked_embpos_gelu_e_kernel(tc, xT, w1, w2_words, w2_scales, pos, offs, out):
     nc = tc.nc
     with ExitStack() as ctx:
         keep = ctx.enter_context(tc.tile_pool(name="keep", bufs=1))
-        reused = ctx.enter_context(tc.tile_pool(name="reused", bufs=1))
         psum = ctx.enter_context(tc.psum_pool(name="psum", bufs=1))
 
         offsets = keep.tile([P, S // STRIPE], U16, name="offsets")
@@ -59,7 +68,7 @@ def tile_picked_embpos_gelu_e_kernel(tc, xT, w1, w2_words, w2_scales, pos, offs,
             rows = xT[z * K_PASS:(z + 1) * K_PASS, :].rearrange("(p j) c -> p j c", j=PACK)
             c0 = 0
             for i, (width, scalar_cols) in enumerate(loads):
-                raw = keep.tile([P, 2, width], F32, name="x_raw_%d_%d" % (pair, i))
+                raw = keep.tile([P, 2, width], F32, name="x_raw_%d_%d" % (pair, i), align_bytes=64)
                 nc.sync.dma_start(out=raw[:], in_=rows[:, 2 * u:2 * u + 2, c0:c0 + width])
                 x_raw[pair, i] = raw
                 c0 = c0 + width
@@ -71,10 +80,7 @@ def tile_picked_embpos_gelu_e_kernel(tc, xT, w1, w2_words, w2_scales, pos, offs,
             rows = w1[z * K_PASS:(z + 1) * K_PASS, :].rearrange("(p j) c -> p j c", j=PACK)
             c0 = 0
             for i, (width, scalar_cols) in enumerate(W_LOADS[z]):
-                if z == PASSES - 1 and i == len(W_LOADS[z]) - 1:
-                    raw = reused.tile([P, PACK, width], F32, name="w_raw_last", offset=0, align_bytes=64)
-                else:
-                    raw = keep.tile([P, PACK, width], F32, name="w_raw_%d_%d" % (z, i))
+                raw = keep.tile([P, PACK, width], F32, name="w_raw_%d_%d" % (z, i), align_bytes=64)
                 nc.sync.dma_start(out=raw[:], in_=rows[:, :, c0:c0 + width])
                 w_raw[z, i] = raw
                 c0 = c0 + width
@@ -82,22 +88,29 @@ def tile_picked_embpos_gelu_e_kernel(tc, xT, w1, w2_words, w2_scales, pos, offs,
         w2_codes = keep.tile([P, N], U32, name="w2_codes", align_bytes=64)
         w2_bytes = keep.tile([P, N], U8, name="w2_bytes", align_bytes=64)
         nc.vector.memset(w2_bytes[:].bitcast(I32), 0)
-        for q in range(P // QUADRANT):
-            nc.sync.dma_start(out=w2_bytes[QUADRANT * q:QUADRANT * q + 4, :].bitcast(I32),
-                              in_=w2_scales[0, 4 * q:4 * q + 4, :].bitcast(I32))
-        nc.sync.dma_start(out=w2_codes[:].bitcast(I32), in_=w2_words[0].rearrange("p n r -> p (n r)").bitcast(I32))
+
+        def load_w2():
+            for q in range(P // QUADRANT):
+                nc.sync.dma_start(out=w2_bytes[QUADRANT * q:QUADRANT * q + 4, :].bitcast(I32),
+                                  in_=w2_scales[0, 4 * q:4 * q + 4, :].bitcast(I32))
+            nc.sync.dma_start(out=w2_codes[:].bitcast(I32), in_=w2_words[0].rearrange("p n r -> p (n r)").bitcast(I32))
 
         pos_rows = pos.rearrange("(p t) s -> p t s", t=PACK)
-        pos_of_group = []
-        for s0 in range(0, S, POS_LOAD):
-            raw = keep.tile([P, PACK, POS_LOAD], F32, name="pos_%d" % s0, tag="pos_%d" % s0, align_bytes=64)
-            nc.sync.dma_start(out=raw[:], in_=pos_rows[:, :, s0:s0 + POS_LOAD])
-            for a in range(0, POS_LOAD, GROUP):
-                pos_of_group.append(raw[:, :, a:a + GROUP])
+        pos_raw = []
+        for i, s0 in enumerate(starts(POS_LOADS)):
+            if i == 9:
+                load_w2()
+            raw = keep.tile([P, PACK, POS_LOADS[i]], F32, name="pos_%d" % i, align_bytes=64)
+            nc.sync.dma_start(out=raw[:], in_=pos_rows[:, :, s0:s0 + POS_LOADS[i]])
+            pos_raw.append(raw)
+        load_w2()
 
         windows = {}
-        gathered = {}
-        woven = {}
+        gathered = []
+        woven = []
+        for z in range(PASSES):
+            gathered.append(keep.tile([P, 2, S], U32, name="gathered_%d" % z, align_bytes=64))
+            woven.append(keep.tile([P, S, 2], I32, name="woven_%d" % z, align_bytes=64))
         x_codes = {}
         x_bytes = {}
 
@@ -114,89 +127,79 @@ def tile_picked_embpos_gelu_e_kernel(tc, xT, w1, w2_words, w2_scales, pos, offs,
                 c0 = c0 + width
             windows[z, u] = pairs[:].rearrange("p c e -> p (c e)").bitcast(U32)
 
-        def gather(z, u, piece):
-            s0, n = PIECES[z][piece]
-            if (z, piece) not in gathered:
-                gathered[z, piece] = keep.tile([P, 2, n], U32, name="gathered_%d_%d" % (z, piece), align_bytes=64)[:]
-            nc.vector.tensor_copy(out=gathered[z, piece][:, u, :],
+        def gather(z, u, s0, n):
+            nc.vector.tensor_copy(out=gathered[z][:, u, s0:s0 + n],
                                   in_=windows[z, u].indirect(offsets[:, s0 // STRIPE:(s0 + n) // STRIPE]))
 
-        def weave(z, piece):
-            n = PIECES[z][piece][1]
-            woven[z, piece] = keep.tile([P, n, 2], I32, name="woven_%d_%d" % (z, piece), align_bytes=64)
-            nc.vector.tensor_copy(out=woven[z, piece][:], in_=gathered[z, piece].bitcast(I32).rearrange("p u c -> p c u"))
+        def weave(z, s0, n):
+            nc.vector.tensor_copy(out=woven[z][:, s0:s0 + n, :],
+                                  in_=gathered[z][:, :, s0:s0 + n].bitcast(I32).rearrange("p u c -> p c u"))
 
-        def quantise_x(z, piece):
+        def quantise_x(z, piece, behind=None):
             s0, n = PIECES[z][piece]
-            if (z, piece) == (1, LAST_PIECE):
-                codes = reused.tile([P, n], U32, name="x_codes_last", offset=0, align_bytes=64)
-            else:
-                codes = keep.tile([P, n], U32, name="x_codes_%d_%d" % (z, piece), align_bytes=64)
+            name = "x_codes_%d_%d" % (z, piece)
+            codes = keep.tile([P, n], U32, name=name, tag=behind or name, align_bytes=64)
             scales = keep.tile([P, n], U8, name="x_bytes_%d_%d" % (z, piece), align_bytes=64)
             nc.vector.quantize_mx(out=codes[:].bitcast(FP8X4), scales=scales[:],
-                                  in_=woven[z, piece][:].rearrange("p c u -> p (c u)").bitcast(BF16))
+                                  in_=woven[z][:, s0:s0 + n, :].rearrange("p c u -> p (c u)").bitcast(BF16))
             for a in range(0, n, GROUP):
                 x_codes[z, (s0 + a) // GROUP] = codes[:, a:a + GROUP]
                 x_bytes[z, (s0 + a) // GROUP] = scales[:, a:a + GROUP]
             return codes, scales
 
-        for u in range(2):
-            round_pair(0, u)
-            for piece in range(len(PIECES[0])):
-                gather(0, u, piece)
-        weave(0, 0)
-        weave(0, 1)
+        held = len(PIECES[0]) - 1
+        round_pair(0, 0)
+        gather(0, 0, 0, S)
+        round_pair(0, 1)
+        for s0 in (0, HALF):
+            gather(0, 1, s0, HALF)
+        for s0 in (0, HALF):
+            weave(0, s0, HALF)
         first_codes, first_bytes = quantise_x(0, 0)
-        quantise_x(0, 1)
-
-        shared = keep.tile([P, 2 * HALF], U32, name="gathered_shared", align_bytes=64)
-        gathered[1, LAST_PIECE] = shared[:].rearrange("p (u c) -> p u c", u=2)
-        gathered[1, 0] = shared[:, HALF:2 * HALF].rearrange("p (u c) -> p u c", u=2)
+        for piece in range(1, held):
+            quantise_x(0, piece)
         round_pair(1, 0)
-        for piece in range(len(PIECES[1])):
-            gather(1, 0, piece)
+        gather(1, 0, 0, S)
         round_pair(1, 1)
+        for i, s0 in enumerate(starts(LAST_GATHERS)):
+            if i == 1:
+                quantise_x(0, held, behind="x_raw_%d_%d" % HOLD_X_LOAD)
+            gather(1, 1, s0, LAST_GATHERS[i])
+        for s0 in (0, HALF):
+            weave(1, s0, HALF)
 
         unread = psum.tile([P, HALF], F32, name="unread", tag="bank_%d" % (BANKS - 1))
-
-        def warm_up(g):
-            nc.tensor.matmul_mx(out=unread[:], lhsT=x_codes[1, g].bitcast(FP8X4), lhsT_scale=x_bytes[1, g],
+        held_group = PIECES[0][held][0] // GROUP
+        for repeat in range(WARM_UPS):
+            nc.tensor.matmul_mx(out=unread[:], lhsT=x_codes[0, held_group].bitcast(FP8X4), lhsT_scale=x_bytes[0, held_group],
                                 rhs=first_codes[:].bitcast(FP8X4), rhs_scale=first_bytes[:], start=True, stop=True)
 
-        gather(1, 1, 0)
-        gather(1, 1, 1)
-        weave(1, 0)
-        weave(1, 1)
-        quantise_x(1, 0)
-        for repeat in range(EARLY_WARM_UPS):
-            warm_up(0)
-        gather(1, 1, LAST_PIECE)
-        quantise_x(1, 1)
-        warm_up(PIECES[1][1][0] // GROUP)
-        weave(1, LAST_PIECE)
-
+        w_rounded = []
         w_codes = []
         w_bytes = []
+        for z in range(PASSES):
+            w_rounded.append(keep.tile([P, PACK, P, PACK], BF16, name="w_rounded_%d" % z, align_bytes=64))
+            w_codes.append(keep.tile([P, H], U32, name="w_codes_%d" % z, align_bytes=64))
+            w_bytes.append(keep.tile([P, H], U8, name="w_bytes_%d" % z, align_bytes=64))
 
-        def quantise_w1(z):
-            rounded = keep.tile([P, PACK, P, PACK], BF16, name="w_rounded_%d" % z, align_bytes=64)
-            dst = rounded[:].rearrange("p t m j -> p m j t")
-            m0 = 0
-            for i, (width, scalar_cols) in enumerate(W_LOADS[z]):
-                src = w_raw[z, i][:].rearrange("p j (m t) -> p m j t", t=PACK)
-                m_all, m_scalar = width // PACK, scalar_cols // PACK
+        def round_w1(z, i):
+            width, scalar_cols = W_LOADS[z][i]
+            m0 = sum(load[0] for load in W_LOADS[z][:i]) // PACK
+            dst = w_rounded[z][:].rearrange("p t m j -> p m j t")
+            src = w_raw[z, i][:].rearrange("p j (m t) -> p m j t", t=PACK)
+            m_all, m_scalar = width // PACK, scalar_cols // PACK
+            if m_scalar > 0:
                 nc.scalar.activation(out=dst[:, m0:m0 + m_scalar], in_=src[:, 0:m_scalar], func=COPY)
-                if m_scalar < m_all:
-                    nc.vector.tensor_copy(out=dst[:, m0 + m_scalar:m0 + m_all], in_=src[:, m_scalar:m_all])
-                m0 = m0 + m_all
-            codes = keep.tile([P, H], U32, name="w_codes_%d" % z, align_bytes=64)
-            scales = keep.tile([P, H], U8, name="w_bytes_%d" % z, align_bytes=64)
-            step = H // W_CALLS[z]
-            for c in range(0, H, step):
-                nc.vector.quantize_mx(out=codes[:, c:c + step].bitcast(FP8X4), scales=scales[:, c:c + step],
-                                      in_=rounded[:].rearrange("p t m j -> p (t m j)")[:, PACK * c:PACK * (c + step)])
-            w_codes.append(codes)
-            w_bytes.append(scales)
+            if m_scalar < m_all:
+                nc.vector.tensor_copy(out=dst[:, m0 + m_scalar:m0 + m_all], in_=src[:, m_scalar:m_all])
+
+        def quantise_w1(z, part):
+            tiles, parts = W_SPLIT[z]
+            width = tiles * P // parts
+            for t0 in range(0, PACK, tiles):
+                c = t0 * P + part * width
+                nc.vector.quantize_mx(out=w_codes[z][:, c:c + width].bitcast(FP8X4), scales=w_bytes[z][:, c:c + width],
+                                      in_=w_rounded[z][:].rearrange("p t m j -> p (t m j)")[:, PACK * c:PACK * (c + width)])
 
         acc = {}
 
@@ -209,68 +212,77 @@ def tile_picked_embpos_gelu_e_kernel(tc, xT, w1, w2_words, w2_scales, pos, offs,
                 lhsT_scale=w_bytes[z][:, t * P:(t + 1) * P],
                 rhs=x_codes[z, g].bitcast(FP8X4),
                 rhs_scale=x_bytes[z, g],
-                start=(z == 0), stop=(z == PASSES - 1))
+                start=(z == 0 and t == 0), stop=(z == PASSES - 1 and t == PACK - 1))
 
         def finish_first_product(g):
-            if g >= RING:
-                product_pass(g, 0, 0)
-            product_pass(g, 0, 1)
-            for t in range(1, PACK):
-                for z in range(PASSES):
+            for z in range(0 if g >= RING else 1, PASSES):
+                for t in range(PACK):
                     product_pass(g, t, z)
 
-        quantise_w1(0)
-        for g in range(RING):
-            product_pass(g, 0, 0)
-        quantise_w1(1)
-        quantise_x(1, LAST_PIECE)
+        for i in range(len(W_LOADS[0])):
+            round_w1(0, i)
+        quantise_w1(0, 0)
+        for t in range(PACK):
+            for g in range(RING):
+                product_pass(g, t, 0)
+        for i in range(len(W_LOADS[1])):
+            round_w1(1, i)
+        quantise_x(1, 0, behind="w_raw_0_%d" % (len(W_LOADS[0]) - 1))
+        quantise_w1(1, 0)
+        quantise_x(1, 1, behind="w_raw_1_%d" % (len(W_LOADS[1]) - 1))
         for g in range(RING):
             finish_first_product(g)
 
-        hidden = {}
-        h_code_tiles = {}
+        hidden = keep.tile([P, S, PACK], BF16, name="hidden", align_bytes=64)
+        last_pos = len(POS_LOADS) - 1
+        h_codes = {}
+        h_bytes = keep.tile([P, S], U8, name="h_bytes", align_bytes=64)
 
-        def add_pos_and_gelu(r, i):
-            g = RUNS[r][i]
-            pre = keep.tile([P, PACK, GROUP], F32, name="pre_%d" % g)
-            nc.vector.tensor_tensor(out=pre[:], in0=acc[g][:], in1=pos_of_group[g], op=ADD)
-            if i == 0:
-                hidden[r] = keep.tile([P, GROUP * len(RUNS[r]), PACK], BF16, name="hidden_%d" % r, align_bytes=64)
+        def add_pos_and_gelu(s0, n):
+            g, a = divmod(s0, GROUP)
+            load = max(i for i, first in enumerate(starts(POS_LOADS)) if first <= s0)
+            b = s0 - starts(POS_LOADS)[load]
+            pre = keep.tile([P, PACK, n], F32, name="pre_%d" % s0, align_bytes=64)
+            nc.vector.tensor_tensor(out=pre[:], in0=acc[g][:, :, a:a + n], in1=pos_raw[load][:, :, b:b + n], op=ADD)
             nc.scalar.activation(
-                out=hidden[r][:, i * GROUP:(i + 1) * GROUP, :].rearrange("p (c e) t -> p c t e", e=4),
+                out=hidden[:, s0:s0 + n, :].rearrange("p (c e) t -> p c t e", e=4),
                 in_=pre[:].rearrange("p t (c e) -> p c t e", e=4), func=GELU)
 
-        def second_product(r):
-            s0 = RUNS[r][0] * GROUP
-            n = GROUP * len(RUNS[r])
-            if r == 0:
-                h_code_tiles["first"] = keep.tile([P, n], U32, name="h_codes_first", tag="pos_%d" % (S - 2 * POS_LOAD), align_bytes=64)
-                h_codes = h_code_tiles["first"][:]
-            else:
-                if r == 1:
-                    h_code_tiles["rest"] = keep.tile([P, S], U32, name="h_codes_rest", tag="pos_%d" % (S - POS_LOAD), align_bytes=64)
-                h_codes = h_code_tiles["rest"][:, s0:s0 + n]
-            h_bytes = keep.tile([P, n], U8, name="h_bytes_%d" % r, align_bytes=64)
-            nc.vector.quantize_mx(out=h_codes.bitcast(FP8X4), scales=h_bytes[:], in_=hidden[r][:].rearrange("p c t -> p (c t)"))
-            sums = psum.tile([P, n], F32, name="sums_%d" % r, tag="bank_%d" % (RING + r % (BANKS - RING)))
+        def quantise_h(i):
+            s0, n = starts(H_CALLS)[i], H_CALLS[i]
+            which = 0
+            if which not in h_codes:
+                h_codes[which] = keep.tile([P, S], U32, name="h_codes", tag="pre_%d" % HOLD_STEP, align_bytes=64)
+            nc.vector.quantize_mx(out=h_codes[which][:, s0:s0 + n].bitcast(FP8X4), scales=h_bytes[:, s0:s0 + n],
+                                  in_=hidden[:, s0:s0 + n, :].rearrange("p c t -> p (c t)"))
+            return h_codes[which]
+
+        def second_product(r, codes):
+            s0, n = starts(RUNS)[r], RUNS[r]
+            sums = psum.tile([P, n], F32, name="sums_%d" % r, tag="bank_%d" % RUN_BANKS[r])
             nc.tensor.matmul_mx(out=sums[:], lhsT=w2_codes[:].bitcast(FP8X4), lhsT_scale=w2_bytes[:],
-                                rhs=h_codes.bitcast(FP8X4), rhs_scale=h_bytes[:], start=True, stop=True)
+                                rhs=codes[:, s0:s0 + n].bitcast(FP8X4), rhs_scale=h_bytes[:, s0:s0 + n], start=True, stop=True)
             result = keep.tile([P, n], F32, name="result_%d" % r)
-            if r == VECTOR_RUN:
+            if r in VECTOR_RUNS:
                 nc.vector.tensor_copy(out=result[:], in_=sums[:])
             else:
                 nc.scalar.activation(out=result[:], in_=sums[:], func=COPY)
             queue = nc.scalar if r == len(RUNS) - 1 else nc.sync
             queue.dma_start(out=out[:, s0:s0 + n], in_=result[:])
 
-        last_group_of_third_load = (S - POS_LOAD) // GROUP - 1
-        for g in range(GROUPS):
-            for r, run in enumerate(RUNS):
-                if g in run:
-                    add_pos_and_gelu(r, run.index(g))
-            if g + RING < GROUPS:
-                finish_first_product(g + RING)
-            if g == last_group_of_third_load:
-                second_product(0)
-        for r in range(1, len(RUNS)):
-            second_product(r)
+        def finish_calls(calls):
+            for i in calls:
+                codes = quantise_h(i)
+                end = starts(H_CALLS)[i] + H_CALLS[i]
+                for r, s0 in enumerate(starts(RUNS)):
+                    if s0 + RUNS[r] == end:
+                        second_product(r, codes)
+
+        for i, s0 in enumerate(starts(STEPS)):
+            add_pos_and_gelu(s0, STEPS[i])
+            end = s0 + STEPS[i]
+            if end % GROUP == 0 and end // GROUP - 1 + RING < GROUPS:
+                finish_first_product(end // GROUP - 1 + RING)
+            if end == S - POS_LOADS[last_pos]:
+                finish_calls(range(EARLY_CALLS))
+        finish_calls(range(EARLY_CALLS, len(H_CALLS)))

@@ -24,6 +24,7 @@ HALF = S // 2
 STRIPE = 16
 QUADRANT = 32
 BANKS = 8
+DMA_ALIGN = 256
 
 X_LOADS = (
     ((2048, 704),),
@@ -68,7 +69,7 @@ def tile_picked_embpos_gelu_e_kernel(tc, xT, w1, w2_words, w2_scales, pos, offs,
             rows = xT[z * K_PASS:(z + 1) * K_PASS, :].rearrange("(p j) c -> p j c", j=PACK)
             c0 = 0
             for i, (width, scalar_cols) in enumerate(loads):
-                raw = keep.tile([P, 2, width], F32, name="x_raw_%d_%d" % (pair, i), align_bytes=64)
+                raw = keep.tile([P, 2, width], F32, name="x_raw_%d_%d" % (pair, i), align_bytes=DMA_ALIGN)
                 nc.sync.dma_start(out=raw[:], in_=rows[:, 2 * u:2 * u + 2, c0:c0 + width])
                 x_raw[pair, i] = raw
                 c0 = c0 + width
@@ -80,13 +81,13 @@ def tile_picked_embpos_gelu_e_kernel(tc, xT, w1, w2_words, w2_scales, pos, offs,
             rows = w1[z * K_PASS:(z + 1) * K_PASS, :].rearrange("(p j) c -> p j c", j=PACK)
             c0 = 0
             for i, (width, scalar_cols) in enumerate(W_LOADS[z]):
-                raw = keep.tile([P, PACK, width], F32, name="w_raw_%d_%d" % (z, i), align_bytes=64)
+                raw = keep.tile([P, PACK, width], F32, name="w_raw_%d_%d" % (z, i), align_bytes=DMA_ALIGN)
                 nc.sync.dma_start(out=raw[:], in_=rows[:, :, c0:c0 + width])
                 w_raw[z, i] = raw
                 c0 = c0 + width
 
-        w2_codes = keep.tile([P, N], U32, name="w2_codes", align_bytes=64)
-        w2_bytes = keep.tile([P, N], U8, name="w2_bytes", align_bytes=64)
+        w2_codes = keep.tile([P, N], U32, name="w2_codes", align_bytes=DMA_ALIGN)
+        w2_bytes = keep.tile([P, N], U8, name="w2_bytes", align_bytes=DMA_ALIGN)
         nc.vector.memset(w2_bytes[:].bitcast(I32), 0)
 
         def load_w2():
@@ -100,7 +101,7 @@ def tile_picked_embpos_gelu_e_kernel(tc, xT, w1, w2_words, w2_scales, pos, offs,
         for i, s0 in enumerate(starts(POS_LOADS)):
             if i == 9:
                 load_w2()
-            raw = keep.tile([P, PACK, POS_LOADS[i]], F32, name="pos_%d" % i, align_bytes=64)
+            raw = keep.tile([P, PACK, POS_LOADS[i]], F32, name="pos_%d" % i, align_bytes=DMA_ALIGN)
             nc.sync.dma_start(out=raw[:], in_=pos_rows[:, :, s0:s0 + POS_LOADS[i]])
             pos_raw.append(raw)
         load_w2()
@@ -138,7 +139,7 @@ def tile_picked_embpos_gelu_e_kernel(tc, xT, w1, w2_words, w2_scales, pos, offs,
         def quantise_x(z, piece, behind=None):
             s0, n = PIECES[z][piece]
             name = "x_codes_%d_%d" % (z, piece)
-            codes = keep.tile([P, n], U32, name=name, tag=behind or name, align_bytes=64)
+            codes = keep.tile([P, n], U32, name=name, tag=behind or name, align_bytes=DMA_ALIGN)
             scales = keep.tile([P, n], U8, name="x_bytes_%d_%d" % (z, piece), align_bytes=64)
             nc.vector.quantize_mx(out=codes[:].bitcast(FP8X4), scales=scales[:],
                                   in_=woven[z][:, s0:s0 + n, :].rearrange("p c u -> p (c u)").bitcast(BF16))
@@ -262,7 +263,7 @@ def tile_picked_embpos_gelu_e_kernel(tc, xT, w1, w2_words, w2_scales, pos, offs,
             sums = psum.tile([P, n], F32, name="sums_%d" % r, tag="bank_%d" % RUN_BANKS[r])
             nc.tensor.matmul_mx(out=sums[:], lhsT=w2_codes[:].bitcast(FP8X4), lhsT_scale=w2_bytes[:],
                                 rhs=codes[:, s0:s0 + n].bitcast(FP8X4), rhs_scale=h_bytes[:, s0:s0 + n], start=True, stop=True)
-            result = keep.tile([P, n], F32, name="result_%d" % r)
+            result = keep.tile([P, n], F32, name="result_%d" % r, align_bytes=DMA_ALIGN)
             if r in VECTOR_RUNS:
                 nc.vector.tensor_copy(out=result[:], in_=sums[:])
             else:

@@ -36,15 +36,15 @@ PIECES = (((0, 512), (512, 256), (768, 128), (896, 128)), ((0, 512), (512, 512))
 HOLD_X_LOAD = (3, 3)
 LAST_GATHERS = (256, 256, 512)
 W_LOADS = (((256, 256), (256, 256)), ((256, 256), (128, 0), (128, 128)))
-W_SPLIT = ((2, 1), (2, 1))
+W_SPLIT = ((2, 1), (1, 2))
 POS_LOADS = (256, 256, 256, 256)
 GROUP = 128
 GROUPS = S // GROUP
-RING = 4
+RING = 5
 STEPS = (32, 96, 128, 128, 128, 128, 128, 128, 64, 64)
 H_CALLS = (256, 256, 256, 128, 64, 64)
 RUNS = (256, 256, 256, 128, 128)
-RUN_BANKS = (4, 5, 6, 7, 4)
+RUN_BANKS = (5, 6, 7, 3, 4)
 VECTOR_RUNS = (2,)
 EARLY_CALLS = 0
 HOLD_STEP = 640
@@ -226,10 +226,12 @@ def tile_picked_embpos_gelu_e_kernel(tc, xT, w1, w2_words, w2_scales, pos, offs,
         for t in range(PACK):
             for g in range(RING):
                 product_pass(g, t, 0)
-        for i in range(len(W_LOADS[1])):
-            round_w1(1, i)
+        round_w1(1, 0)
+        round_w1(1, 1)
         quantise_x(1, 0, behind="w_raw_0_%d" % (len(W_LOADS[0]) - 1))
         quantise_w1(1, 0)
+        round_w1(1, 2)
+        quantise_w1(1, 1)
         quantise_x(1, 1, behind="w_raw_1_%d" % (len(W_LOADS[1]) - 1))
         for g in range(RING):
             finish_first_product(g)

@@ -23,31 +23,32 @@ PASSES = K // K_PASS
 HALF = S // 2
 STRIPE = 16
 QUADRANT = 32
+SCALE_ROWS = 4
 BANKS = 8
+MX_ALIGN = 64
 DMA_ALIGN = 256
 
 X_LOADS = (
-    ((2048, 704),),
-    ((1024, 1024), (768, 0), (256, 256)),
-    ((512, 512), (512, 512), (512, 512), (512, 512)),
-    ((768, 768), (768, 512), (256, 0), (256, 128)),
+    ((1536, 512), (512, 176)),
+    ((1536, 512), (512, 176)),
+    ((512, 512), (512, 512), (512, 512), (512, 384)),
+    ((512, 512), (512, 512), (512, 512), (256, 0), (256, 88)),
 )
-PIECES = (((0, 512), (512, 256), (768, 128), (896, 128)), ((0, 512), (512, 512)))
-HOLD_X_LOAD = (3, 3)
-LAST_GATHERS = (256, 256, 512)
-W_LOADS = (((256, 256), (256, 256)), ((256, 256), (128, 0), (128, 128)))
-W_SPLIT = ((2, 1), (1, 2))
-POS_LOADS = (256, 256, 256, 256)
+W_LOAD = 128
+W_LOADS = H // W_LOAD
+W_SHARED_LOAD = (PASSES - 1, W_LOADS - 1)
+W_VECTOR_COLUMNS = 64
+W2_WORDS_BEHIND = (0, 1)
 GROUP = 128
 GROUPS = S // GROUP
-RING = 5
-STEPS = (32, 96, 128, 128, 128, 128, 128, 128, 64, 64)
+RING = 4
+STEPS = (32, 96) + (GROUP,) * (GROUPS - 2) + (64, 64)
 H_CALLS = (256, 256, 256, 128, 64, 64)
 RUNS = (256, 256, 256, 128, 128)
-RUN_BANKS = (5, 6, 7, 3, 4)
-VECTOR_RUNS = (2,)
-EARLY_CALLS = 0
-HOLD_STEP = 640
+VECTOR_RUN = 2
+FIRST_H_CALL_AT = S - GROUP
+FIRST_H_CALL_BEHIND = 4 * GROUP
+LATER_H_CALLS_BEHIND = 5 * GROUP
 WARM_UPS = 4
 
 
@@ -76,48 +77,44 @@ def tile_picked_embpos_gelu_e_kernel(tc, xT, w1, w2_words, w2_scales, pos, offs,
             if pair == 0:
                 nc.sync.dma_start(offsets[:], offs)
 
-        w_raw = {}
-        for z in range(PASSES):
-            rows = w1[z * K_PASS:(z + 1) * K_PASS, :].rearrange("(p j) c -> p j c", j=PACK)
-            c0 = 0
-            for i, (width, scalar_cols) in enumerate(W_LOADS[z]):
-                raw = keep.tile([P, PACK, width], F32, name="w_raw_%d_%d" % (z, i), align_bytes=DMA_ALIGN)
-                nc.sync.dma_start(out=raw[:], in_=rows[:, :, c0:c0 + width])
-                w_raw[z, i] = raw
-                c0 = c0 + width
-
         w2_codes = keep.tile([P, N], U32, name="w2_codes", align_bytes=DMA_ALIGN)
         w2_bytes = keep.tile([P, N], U8, name="w2_bytes", align_bytes=DMA_ALIGN)
         nc.vector.memset(w2_bytes[:].bitcast(I32), 0)
 
-        def load_w2():
-            for q in range(P // QUADRANT):
-                nc.sync.dma_start(out=w2_bytes[QUADRANT * q:QUADRANT * q + 4, :].bitcast(I32),
-                                  in_=w2_scales[0, 4 * q:4 * q + 4, :].bitcast(I32))
-            nc.sync.dma_start(out=w2_codes[:].bitcast(I32), in_=w2_words[0].rearrange("p n r -> p (n r)").bitcast(I32))
+        w_raw = {}
+        for z in range(PASSES):
+            rows = w1[z * K_PASS:(z + 1) * K_PASS, :].rearrange("(p j) c -> p j c", j=PACK)
+            for i in range(W_LOADS):
+                raw = keep.tile([P, PACK, W_LOAD], F32, name="w_raw_%d_%d" % (z, i), align_bytes=DMA_ALIGN)
+                nc.sync.dma_start(out=raw[:], in_=rows[:, :, i * W_LOAD:(i + 1) * W_LOAD])
+                w_raw[z, i] = raw
+                if (z, i) == W2_WORDS_BEHIND:
+                    nc.sync.dma_start(out=w2_codes[:].bitcast(I32),
+                                      in_=w2_words[0].rearrange("p n r -> p (n r)").bitcast(I32))
 
         pos_rows = pos.rearrange("(p t) s -> p t s", t=PACK)
         pos_raw = []
-        for i, s0 in enumerate(starts(POS_LOADS)):
-            if i == 9:
-                load_w2()
-            raw = keep.tile([P, PACK, POS_LOADS[i]], F32, name="pos_%d" % i, align_bytes=DMA_ALIGN)
-            nc.sync.dma_start(out=raw[:], in_=pos_rows[:, :, s0:s0 + POS_LOADS[i]])
+        for g in range(GROUPS):
+            raw = keep.tile([P, PACK, GROUP], F32, name="pos_%d" % g, align_bytes=DMA_ALIGN)
+            nc.sync.dma_start(out=raw[:], in_=pos_rows[:, :, g * GROUP:(g + 1) * GROUP])
             pos_raw.append(raw)
-        load_w2()
+
+        for q in range(P // QUADRANT):
+            nc.sync.dma_start(out=w2_bytes[QUADRANT * q:QUADRANT * q + SCALE_ROWS, :].bitcast(I32),
+                              in_=w2_scales[0, SCALE_ROWS * q:SCALE_ROWS * (q + 1), :].bitcast(I32))
 
         windows = {}
         gathered = []
         woven = []
         for z in range(PASSES):
-            gathered.append(keep.tile([P, 2, S], U32, name="gathered_%d" % z, align_bytes=64))
-            woven.append(keep.tile([P, S, 2], I32, name="woven_%d" % z, align_bytes=64))
+            gathered.append(keep.tile([P, 2, S], U32, name="gathered_%d" % z, align_bytes=MX_ALIGN))
+            woven.append(keep.tile([P, S, 2], I32, name="woven_%d" % z, align_bytes=MX_ALIGN))
         x_codes = {}
         x_bytes = {}
 
         def round_pair(z, u):
             pair = 2 * z + u
-            pairs = keep.tile([P, T, 2], BF16, name="pairs_%d" % pair, align_bytes=64)
+            pairs = keep.tile([P, T, 2], BF16, name="pairs_%d" % pair, align_bytes=MX_ALIGN)
             c0 = 0
             for i, (width, scalar_cols) in enumerate(X_LOADS[pair]):
                 src = x_raw[pair, i][:].rearrange("p e c -> p c e")
@@ -132,75 +129,58 @@ def tile_picked_embpos_gelu_e_kernel(tc, xT, w1, w2_words, w2_scales, pos, offs,
             nc.vector.tensor_copy(out=gathered[z][:, u, s0:s0 + n],
                                   in_=windows[z, u].indirect(offsets[:, s0 // STRIPE:(s0 + n) // STRIPE]))
 
-        def weave(z, s0, n):
-            nc.vector.tensor_copy(out=woven[z][:, s0:s0 + n, :],
-                                  in_=gathered[z][:, :, s0:s0 + n].bitcast(I32).rearrange("p u c -> p c u"))
+        def look_up(z):
+            round_pair(z, 0)
+            gather(z, 0, 0, S)
+            round_pair(z, 1)
+            for s0 in (0, HALF):
+                gather(z, 1, s0, HALF)
+            for s0 in (0, HALF):
+                nc.vector.tensor_copy(out=woven[z][:, s0:s0 + HALF, :],
+                                      in_=gathered[z][:, :, s0:s0 + HALF].bitcast(I32).rearrange("p u c -> p c u"))
 
-        def quantise_x(z, piece, behind=None):
-            s0, n = PIECES[z][piece]
-            name = "x_codes_%d_%d" % (z, piece)
-            codes = keep.tile([P, n], U32, name=name, tag=behind or name, align_bytes=DMA_ALIGN)
-            scales = keep.tile([P, n], U8, name="x_bytes_%d_%d" % (z, piece), align_bytes=64)
+        def quantise_x(z, half, behind=None):
+            s0 = half * HALF
+            name = "x_codes_%d_%d" % (z, half)
+            codes = keep.tile([P, HALF], U32, name=name, tag=behind or name, align_bytes=DMA_ALIGN)
+            scales = keep.tile([P, HALF], U8, name="x_bytes_%d_%d" % (z, half), align_bytes=MX_ALIGN)
             nc.vector.quantize_mx(out=codes[:].bitcast(FP8X4), scales=scales[:],
-                                  in_=woven[z][:, s0:s0 + n, :].rearrange("p c u -> p (c u)").bitcast(BF16))
-            for a in range(0, n, GROUP):
+                                  in_=woven[z][:, s0:s0 + HALF, :].rearrange("p c u -> p (c u)").bitcast(BF16))
+            for a in range(0, HALF, GROUP):
                 x_codes[z, (s0 + a) // GROUP] = codes[:, a:a + GROUP]
                 x_bytes[z, (s0 + a) // GROUP] = scales[:, a:a + GROUP]
             return codes, scales
 
-        held = len(PIECES[0]) - 1
-        round_pair(0, 0)
-        gather(0, 0, 0, S)
-        round_pair(0, 1)
-        for s0 in (0, HALF):
-            gather(0, 1, s0, HALF)
-        for s0 in (0, HALF):
-            weave(0, s0, HALF)
+        look_up(0)
         first_codes, first_bytes = quantise_x(0, 0)
-        for piece in range(1, held):
-            quantise_x(0, piece)
-        round_pair(1, 0)
-        gather(1, 0, 0, S)
-        round_pair(1, 1)
-        for i, s0 in enumerate(starts(LAST_GATHERS)):
-            if i == 1:
-                quantise_x(0, held, behind="x_raw_%d_%d" % HOLD_X_LOAD)
-            gather(1, 1, s0, LAST_GATHERS[i])
-        for s0 in (0, HALF):
-            weave(1, s0, HALF)
+        quantise_x(0, 1)
+        look_up(1)
 
         unread = psum.tile([P, HALF], F32, name="unread", tag="bank_%d" % (BANKS - 1))
-        held_group = PIECES[0][held][0] // GROUP
         for repeat in range(WARM_UPS):
-            nc.tensor.matmul_mx(out=unread[:], lhsT=x_codes[0, held_group].bitcast(FP8X4), lhsT_scale=x_bytes[0, held_group],
+            nc.tensor.matmul_mx(out=unread[:], lhsT=w2_codes[:].bitcast(FP8X4), lhsT_scale=x_bytes[0, 0],
                                 rhs=first_codes[:].bitcast(FP8X4), rhs_scale=first_bytes[:], start=True, stop=True)
 
         w_rounded = []
-        w_codes = []
+        w_codes = {}
         w_bytes = []
         for z in range(PASSES):
-            w_rounded.append(keep.tile([P, PACK, P, PACK], BF16, name="w_rounded_%d" % z, align_bytes=64))
-            w_codes.append(keep.tile([P, H], U32, name="w_codes_%d" % z, align_bytes=64))
-            w_bytes.append(keep.tile([P, H], U8, name="w_bytes_%d" % z, align_bytes=64))
+            w_rounded.append(keep.tile([P, PACK, P, PACK], BF16, name="w_rounded_%d" % z, align_bytes=MX_ALIGN))
+            w_bytes.append(keep.tile([P, H], U8, name="w_bytes_%d" % z, align_bytes=MX_ALIGN))
 
         def round_w1(z, i):
-            width, scalar_cols = W_LOADS[z][i]
-            m0 = sum(load[0] for load in W_LOADS[z][:i]) // PACK
-            dst = w_rounded[z][:].rearrange("p t m j -> p m j t")
+            m_all = W_LOAD // PACK
+            m_scalar = m_all - W_VECTOR_COLUMNS // PACK if (z, i) == W_SHARED_LOAD else m_all
+            dst = w_rounded[z][:].rearrange("p t m j -> p m j t")[:, i * m_all:(i + 1) * m_all]
             src = w_raw[z, i][:].rearrange("p j (m t) -> p m j t", t=PACK)
-            m_all, m_scalar = width // PACK, scalar_cols // PACK
-            if m_scalar > 0:
-                nc.scalar.activation(out=dst[:, m0:m0 + m_scalar], in_=src[:, 0:m_scalar], func=COPY)
+            nc.scalar.activation(out=dst[:, 0:m_scalar], in_=src[:, 0:m_scalar], func=COPY)
             if m_scalar < m_all:
-                nc.vector.tensor_copy(out=dst[:, m0 + m_scalar:m0 + m_all], in_=src[:, m_scalar:m_all])
+                nc.vector.tensor_copy(out=dst[:, m_scalar:m_all], in_=src[:, m_scalar:m_all])
 
-        def quantise_w1(z, part):
-            tiles, parts = W_SPLIT[z]
-            width = tiles * P // parts
-            for t0 in range(0, PACK, tiles):
-                c = t0 * P + part * width
-                nc.vector.quantize_mx(out=w_codes[z][:, c:c + width].bitcast(FP8X4), scales=w_bytes[z][:, c:c + width],
-                                      in_=w_rounded[z][:].rearrange("p t m j -> p (t m j)")[:, PACK * c:PACK * (c + width)])
+        def quantise_w1(z, c0, width):
+            values = w_rounded[z][:].rearrange("p t m j -> p (t m j)")
+            nc.vector.quantize_mx(out=w_codes[z][:, c0:c0 + width].bitcast(FP8X4), scales=w_bytes[z][:, c0:c0 + width],
+                                  in_=values[:, PACK * c0:PACK * (c0 + width)])
 
         acc = {}
 
@@ -216,76 +196,78 @@ def tile_picked_embpos_gelu_e_kernel(tc, xT, w1, w2_words, w2_scales, pos, offs,
                 start=(z == 0 and t == 0), stop=(z == PASSES - 1 and t == PACK - 1))
 
         def finish_first_product(g):
-            for z in range(0 if g >= RING else 1, PASSES):
+            for z in range(1 if g < RING else 0, PASSES):
                 for t in range(PACK):
                     product_pass(g, t, z)
 
-        for i in range(len(W_LOADS[0])):
+        last = W_LOADS - 1
+        for i in range(W_LOADS):
             round_w1(0, i)
-        quantise_w1(0, 0)
+        w_codes[0] = keep.tile([P, H], U32, name="w_codes_0", align_bytes=DMA_ALIGN)
+        for c0 in (0, H // 2):
+            quantise_w1(0, c0, H // 2)
         for t in range(PACK):
             for g in range(RING):
                 product_pass(g, t, 0)
-        round_w1(1, 0)
-        round_w1(1, 1)
-        quantise_x(1, 0, behind="w_raw_0_%d" % (len(W_LOADS[0]) - 1))
-        quantise_w1(1, 0)
-        round_w1(1, 2)
-        quantise_w1(1, 1)
-        quantise_x(1, 1, behind="w_raw_1_%d" % (len(W_LOADS[1]) - 1))
+        for i in range(last):
+            round_w1(1, i)
+        quantise_x(1, 0, behind="w_raw_0_%d" % last)
+        round_w1(1, last)
+        w_codes[1] = keep.tile([P, H], U32, name="w_codes_1", tag="w_raw_1_%d" % (last - 1), align_bytes=DMA_ALIGN)
+        for m0 in (0, P // 2):
+            for t in range(PACK):
+                quantise_w1(1, t * P + m0, P // 2)
+        quantise_x(1, 1, behind="w_raw_1_%d" % last)
         for g in range(RING):
             finish_first_product(g)
 
-        hidden = keep.tile([P, S, PACK], BF16, name="hidden", align_bytes=64)
-        last_pos = len(POS_LOADS) - 1
-        h_codes = {}
-        h_bytes = keep.tile([P, S], U8, name="h_bytes", align_bytes=64)
+        hidden = keep.tile([P, S, PACK], BF16, name="hidden", align_bytes=MX_ALIGN)
+        h_bytes = keep.tile([P, S], U8, name="h_bytes", align_bytes=MX_ALIGN)
 
         def add_pos_and_gelu(s0, n):
             g, a = divmod(s0, GROUP)
-            load = max(i for i, first in enumerate(starts(POS_LOADS)) if first <= s0)
-            b = s0 - starts(POS_LOADS)[load]
-            pre = keep.tile([P, PACK, n], F32, name="pre_%d" % s0, align_bytes=64)
-            nc.vector.tensor_tensor(out=pre[:], in0=acc[g][:, :, a:a + n], in1=pos_raw[load][:, :, b:b + n], op=ADD)
+            pre = keep.tile([P, PACK, n], F32, name="pre_%d" % s0, align_bytes=MX_ALIGN)
+            nc.vector.tensor_tensor(out=pre[:], in0=acc[g][:, :, a:a + n], in1=pos_raw[g][:, :, a:a + n], op=ADD)
             nc.scalar.activation(
                 out=hidden[:, s0:s0 + n, :].rearrange("p (c e) t -> p c t e", e=4),
                 in_=pre[:].rearrange("p t (c e) -> p c t e", e=4), func=GELU)
 
-        def quantise_h(i):
-            s0, n = starts(H_CALLS)[i], H_CALLS[i]
-            which = 0
-            if which not in h_codes:
-                h_codes[which] = keep.tile([P, S], U32, name="h_codes", tag="pre_%d" % HOLD_STEP, align_bytes=64)
-            nc.vector.quantize_mx(out=h_codes[which][:, s0:s0 + n].bitcast(FP8X4), scales=h_bytes[:, s0:s0 + n],
+        def codes_of_h(name, behind):
+            return keep.tile([P, S], U32, name=name, tag=behind, align_bytes=MX_ALIGN)
+
+        def quantise_h(call, codes):
+            s0, n = starts(H_CALLS)[call], H_CALLS[call]
+            nc.vector.quantize_mx(out=codes[:, s0:s0 + n].bitcast(FP8X4), scales=h_bytes[:, s0:s0 + n],
                                   in_=hidden[:, s0:s0 + n, :].rearrange("p c t -> p (c t)"))
-            return h_codes[which]
 
         def second_product(r, codes):
             s0, n = starts(RUNS)[r], RUNS[r]
-            sums = psum.tile([P, n], F32, name="sums_%d" % r, tag="bank_%d" % RUN_BANKS[r])
+            sums = psum.tile([P, n], F32, name="sums_%d" % r, tag="bank_%d" % (RING + r % (BANKS - RING)))
             nc.tensor.matmul_mx(out=sums[:], lhsT=w2_codes[:].bitcast(FP8X4), lhsT_scale=w2_bytes[:],
-                                rhs=codes[:, s0:s0 + n].bitcast(FP8X4), rhs_scale=h_bytes[:, s0:s0 + n], start=True, stop=True)
+                                rhs=codes[:, s0:s0 + n].bitcast(FP8X4), rhs_scale=h_bytes[:, s0:s0 + n],
+                                start=True, stop=True)
             result = keep.tile([P, n], F32, name="result_%d" % r, align_bytes=DMA_ALIGN)
-            if r in VECTOR_RUNS:
+            if r == VECTOR_RUN:
                 nc.vector.tensor_copy(out=result[:], in_=sums[:])
             else:
                 nc.scalar.activation(out=result[:], in_=sums[:], func=COPY)
             queue = nc.scalar if r == len(RUNS) - 1 else nc.sync
             queue.dma_start(out=out[:, s0:s0 + n], in_=result[:])
 
-        def finish_calls(calls):
-            for i in calls:
-                codes = quantise_h(i)
-                end = starts(H_CALLS)[i] + H_CALLS[i]
-                for r, s0 in enumerate(starts(RUNS)):
-                    if s0 + RUNS[r] == end:
-                        second_product(r, codes)
-
-        for i, s0 in enumerate(starts(STEPS)):
-            add_pos_and_gelu(s0, STEPS[i])
-            end = s0 + STEPS[i]
+        for s0, n in zip(starts(STEPS), STEPS):
+            add_pos_and_gelu(s0, n)
+            end = s0 + n
             if end % GROUP == 0 and end // GROUP - 1 + RING < GROUPS:
                 finish_first_product(end // GROUP - 1 + RING)
-            if end == S - POS_LOADS[last_pos]:
-                finish_calls(range(EARLY_CALLS))
-        finish_calls(range(EARLY_CALLS, len(H_CALLS)))
+            if end == FIRST_H_CALL_AT:
+                first_h_codes = codes_of_h("h_codes_0", behind="pre_%d" % FIRST_H_CALL_BEHIND)
+                quantise_h(0, first_h_codes)
+
+        second_product(0, first_h_codes)
+        later_h_codes = codes_of_h("h_codes_1", behind="pre_%d" % LATER_H_CALLS_BEHIND)
+        run_ends = [s0 + n for s0, n in zip(starts(RUNS), RUNS)]
+        for call in range(1, len(H_CALLS)):
+            quantise_h(call, later_h_codes)
+            end = starts(H_CALLS)[call] + H_CALLS[call]
+            if end in run_ends:
+                second_product(run_ends.index(end), later_h_codes)

@@ -28,20 +28,15 @@ BANKS = 8
 MX_ALIGN = 64
 DMA_ALIGN = 256
 
-X_LOADS = (
-    ((1536, 512), (512, 176)),
-    ((1536, 512), (512, 176)),
-    ((512, 512), (512, 512), (512, 512), (512, 384)),
-    ((512, 512), (512, 512), (512, 512), (256, 0), (256, 88)),
-)
+VECTOR_ENTRIES = 256
+PIECE = 256
 W_LOAD = 128
 W_LOADS = H // W_LOAD
-W_SHARED_LOAD = (PASSES - 1, W_LOADS - 1)
-W_VECTOR_COLUMNS = 64
-W2_WORDS_BEHIND = (0, 1)
+W_VECTOR_COLUMNS = ((128, 0, 0, 128), (0, 0, 0, 64))
 GROUP = 128
 GROUPS = S // GROUP
 RING = 4
+AHEAD = 3
 STEPS = (32, 96) + (GROUP,) * (GROUPS - 2) + (64, 64)
 H_CALLS = (256, 256, 256, 128, 64, 64)
 RUNS = (256, 256, 256, 128, 128)
@@ -49,7 +44,6 @@ VECTOR_RUN = 2
 FIRST_H_CALL_AT = S - GROUP
 FIRST_H_CALL_BEHIND = 4 * GROUP
 LATER_H_CALLS_BEHIND = 5 * GROUP
-WARM_UPS = 4
 
 
 def starts(widths):
@@ -64,22 +58,24 @@ def tile_picked_embpos_gelu_e_kernel(tc, xT, w1, w2_words, w2_scales, pos, offs,
 
         offsets = keep.tile([P, S // STRIPE], U16, name="offsets")
 
-        x_raw = {}
-        for pair, loads in enumerate(X_LOADS):
-            z, u = divmod(pair, 2)
+        planes = {}
+        for z in range(PASSES):
             rows = xT[z * K_PASS:(z + 1) * K_PASS, :].rearrange("(p j) c -> p j c", j=PACK)
-            c0 = 0
-            for i, (width, scalar_cols) in enumerate(loads):
-                raw = keep.tile([P, 2, width], F32, name="x_raw_%d_%d" % (pair, i), align_bytes=DMA_ALIGN)
-                nc.sync.dma_start(out=raw[:], in_=rows[:, 2 * u:2 * u + 2, c0:c0 + width])
-                x_raw[pair, i] = raw
-                c0 = c0 + width
-            if pair == 0:
-                nc.sync.dma_start(offsets[:], offs)
+            for j in range(PACK):
+                plane = keep.tile([P, T], F32, name="plane_%d_%d" % (z, j), align_bytes=DMA_ALIGN)
+                nc.sync.dma_start(out=plane[:], in_=rows[:, j, :])
+                planes[z, j] = plane
+                if (z, j) == (0, 0):
+                    nc.sync.dma_start(offsets[:], offs)
 
         w2_codes = keep.tile([P, N], U32, name="w2_codes", align_bytes=DMA_ALIGN)
         w2_bytes = keep.tile([P, N], U8, name="w2_bytes", align_bytes=DMA_ALIGN)
         nc.vector.memset(w2_bytes[:].bitcast(I32), 0)
+
+        zero = keep.tile([P, 1], F32, name="zero")
+        nc.vector.memset(zero[:], 0.0)
+        unread_gelu = keep.tile([P, 1], F32, name="unread_gelu")
+        nc.scalar.activation(out=unread_gelu[:], in_=zero[:], func=GELU)
 
         w_raw = {}
         for z in range(PASSES):
@@ -88,9 +84,6 @@ def tile_picked_embpos_gelu_e_kernel(tc, xT, w1, w2_words, w2_scales, pos, offs,
                 raw = keep.tile([P, PACK, W_LOAD], F32, name="w_raw_%d_%d" % (z, i), align_bytes=DMA_ALIGN)
                 nc.sync.dma_start(out=raw[:], in_=rows[:, :, i * W_LOAD:(i + 1) * W_LOAD])
                 w_raw[z, i] = raw
-                if (z, i) == W2_WORDS_BEHIND:
-                    nc.sync.dma_start(out=w2_codes[:].bitcast(I32),
-                                      in_=w2_words[0].rearrange("p n r -> p (n r)").bitcast(I32))
 
         pos_rows = pos.rearrange("(p t) s -> p t s", t=PACK)
         pos_raw = []
@@ -99,67 +92,58 @@ def tile_picked_embpos_gelu_e_kernel(tc, xT, w1, w2_words, w2_scales, pos, offs,
             nc.sync.dma_start(out=raw[:], in_=pos_rows[:, :, g * GROUP:(g + 1) * GROUP])
             pos_raw.append(raw)
 
+        nc.sync.dma_start(out=w2_codes[:].bitcast(I32), in_=w2_words[0].rearrange("p n r -> p (n r)").bitcast(I32))
         for q in range(P // QUADRANT):
             nc.sync.dma_start(out=w2_bytes[QUADRANT * q:QUADRANT * q + SCALE_ROWS, :].bitcast(I32),
                               in_=w2_scales[0, SCALE_ROWS * q:SCALE_ROWS * (q + 1), :].bitcast(I32))
 
-        windows = {}
-        gathered = []
+        picked = []
         woven = []
         for z in range(PASSES):
-            gathered.append(keep.tile([P, 2, S], U32, name="gathered_%d" % z, align_bytes=MX_ALIGN))
-            woven.append(keep.tile([P, S, 2], I32, name="woven_%d" % z, align_bytes=MX_ALIGN))
+            picked.append(keep.tile([P, PACK, S], BF16, name="picked_%d" % z, align_bytes=MX_ALIGN))
+            woven.append(keep.tile([P, S, PACK], BF16, name="woven_%d" % z, align_bytes=MX_ALIGN))
         x_codes = {}
         x_bytes = {}
 
-        def round_pair(z, u):
-            pair = 2 * z + u
-            pairs = keep.tile([P, T, 2], BF16, name="pairs_%d" % pair, align_bytes=MX_ALIGN)
-            c0 = 0
-            for i, (width, scalar_cols) in enumerate(X_LOADS[pair]):
-                src = x_raw[pair, i][:].rearrange("p e c -> p c e")
-                if scalar_cols > 0:
-                    nc.scalar.activation(out=pairs[:, c0:c0 + scalar_cols, :], in_=src[:, 0:scalar_cols, :], func=COPY)
-                if scalar_cols < width:
-                    nc.vector.tensor_copy(out=pairs[:, c0 + scalar_cols:c0 + width, :], in_=src[:, scalar_cols:width, :])
-                c0 = c0 + width
-            windows[z, u] = pairs[:].rearrange("p c e -> p (c e)").bitcast(U32)
+        def looked_up(z, j, s0, n):
+            return planes[z, j][:].indirect(offsets[:, s0 // STRIPE:(s0 + n) // STRIPE])
 
-        def gather(z, u, s0, n):
-            nc.vector.tensor_copy(out=gathered[z][:, u, s0:s0 + n],
-                                  in_=windows[z, u].indirect(offsets[:, s0 // STRIPE:(s0 + n) // STRIPE]))
+        def gather(z, j, order=(1, 2, 3)):
+            nc.vector.tensor_copy(out=woven[z][:, 0:VECTOR_ENTRIES, j], in_=looked_up(z, j, 0, VECTOR_ENTRIES))
+            for piece in order:
+                s0 = piece * PIECE
+                nc.scalar.activation(out=picked[z][:, j, s0:s0 + PIECE], in_=looked_up(z, j, s0, PIECE), func=COPY)
 
-        def look_up(z):
-            round_pair(z, 0)
-            gather(z, 0, 0, S)
-            round_pair(z, 1)
-            for s0 in (0, HALF):
-                gather(z, 1, s0, HALF)
-            for s0 in (0, HALF):
-                nc.vector.tensor_copy(out=woven[z][:, s0:s0 + HALF, :],
-                                      in_=gathered[z][:, :, s0:s0 + HALF].bitcast(I32).rearrange("p u c -> p c u"))
+        def weave(z, j0, j1, s0):
+            nc.vector.tensor_copy(out=woven[z][:, s0:s0 + PIECE, j0:j1],
+                                  in_=picked[z][:, j0:j1, s0:s0 + PIECE].rearrange("p j c -> p c j"))
 
-        def quantise_x(z, half, behind=None):
-            s0 = half * HALF
-            name = "x_codes_%d_%d" % (z, half)
-            codes = keep.tile([P, HALF], U32, name=name, tag=behind or name, align_bytes=DMA_ALIGN)
-            scales = keep.tile([P, HALF], U8, name="x_bytes_%d_%d" % (z, half), align_bytes=MX_ALIGN)
+        def weave_planes(z, j0, j1):
+            for s0 in range(VECTOR_ENTRIES, S, PIECE):
+                weave(z, j0, j1, s0)
+
+        def quantise_x(z, s0, n, behind=None):
+            name = "x_codes_%d_%d" % (z, s0)
+            codes = keep.tile([P, n], U32, name=name, tag=behind or name, align_bytes=DMA_ALIGN)
+            scales = keep.tile([P, n], U8, name="x_bytes_%d_%d" % (z, s0), align_bytes=MX_ALIGN)
             nc.vector.quantize_mx(out=codes[:].bitcast(FP8X4), scales=scales[:],
-                                  in_=woven[z][:, s0:s0 + HALF, :].rearrange("p c u -> p (c u)").bitcast(BF16))
-            for a in range(0, HALF, GROUP):
+                                  in_=woven[z][:, s0:s0 + n, :].rearrange("p c j -> p (c j)"))
+            for a in range(0, n, GROUP):
                 x_codes[z, (s0 + a) // GROUP] = codes[:, a:a + GROUP]
                 x_bytes[z, (s0 + a) // GROUP] = scales[:, a:a + GROUP]
-            return codes, scales
 
-        look_up(0)
-        first_codes, first_bytes = quantise_x(0, 0)
-        quantise_x(0, 1)
-        look_up(1)
-
-        unread = psum.tile([P, HALF], F32, name="unread", tag="bank_%d" % (BANKS - 1))
-        for repeat in range(WARM_UPS):
-            nc.tensor.matmul_mx(out=unread[:], lhsT=w2_codes[:].bitcast(FP8X4), lhsT_scale=x_bytes[0, 0],
-                                rhs=first_codes[:].bitcast(FP8X4), rhs_scale=first_bytes[:], start=True, stop=True)
+        for j in range(PACK):
+            gather(0, j)
+            weave_planes(0, j, j + 1)
+        quantise_x(0, 0, HALF)
+        quantise_x(0, HALF, HALF)
+        gather(1, 0)
+        gather(1, 1)
+        weave_planes(1, 0, 2)
+        gather(1, 2, (1, 3, 2))
+        weave(1, 2, 3, PIECE)
+        weave(1, 2, 3, 3 * PIECE)
+        gather(1, 3, (1, 2))
 
         w_rounded = []
         w_codes = {}
@@ -170,10 +154,11 @@ def tile_picked_embpos_gelu_e_kernel(tc, xT, w1, w2_words, w2_scales, pos, offs,
 
         def round_w1(z, i):
             m_all = W_LOAD // PACK
-            m_scalar = m_all - W_VECTOR_COLUMNS // PACK if (z, i) == W_SHARED_LOAD else m_all
+            m_scalar = m_all - W_VECTOR_COLUMNS[z][i] // PACK
             dst = w_rounded[z][:].rearrange("p t m j -> p m j t")[:, i * m_all:(i + 1) * m_all]
             src = w_raw[z, i][:].rearrange("p j (m t) -> p m j t", t=PACK)
-            nc.scalar.activation(out=dst[:, 0:m_scalar], in_=src[:, 0:m_scalar], func=COPY)
+            if m_scalar > 0:
+                nc.scalar.activation(out=dst[:, 0:m_scalar], in_=src[:, 0:m_scalar], func=COPY)
             if m_scalar < m_all:
                 nc.vector.tensor_copy(out=dst[:, m_scalar:m_all], in_=src[:, m_scalar:m_all])
 
@@ -184,8 +169,9 @@ def tile_picked_embpos_gelu_e_kernel(tc, xT, w1, w2_words, w2_scales, pos, offs,
 
         acc = {}
 
-        def product_pass(g, t, z):
-            if t == 0 and z == 0:
+        def product_pass(g, t, z, stop=False):
+            start = g not in acc
+            if start:
                 acc[g] = psum.tile([P, PACK, GROUP], F32, name="acc_%d" % g, tag="bank_%d" % (g % RING))
             nc.tensor.matmul_mx(
                 out=acc[g][:, t, :],
@@ -193,31 +179,38 @@ def tile_picked_embpos_gelu_e_kernel(tc, xT, w1, w2_words, w2_scales, pos, offs,
                 lhsT_scale=w_bytes[z][:, t * P:(t + 1) * P],
                 rhs=x_codes[z, g].bitcast(FP8X4),
                 rhs_scale=x_bytes[z, g],
-                start=(z == 0 and t == 0), stop=(z == PASSES - 1 and t == PACK - 1))
+                start=start, stop=stop)
 
         def finish_first_product(g):
-            for z in range(1 if g < RING else 0, PASSES):
-                for t in range(PACK):
-                    product_pass(g, t, z)
+            order = list(range(PACK)) if g == 0 else list(reversed(range(PACK)))
+            passes = [(t, 1) for t in order] + [(t, 0) for t in order if g >= AHEAD]
+            for t, z in passes:
+                product_pass(g, t, z, stop=((t, z) == passes[-1]))
 
         last = W_LOADS - 1
         for i in range(W_LOADS):
             round_w1(0, i)
         w_codes[0] = keep.tile([P, H], U32, name="w_codes_0", align_bytes=DMA_ALIGN)
-        for c0 in (0, H // 2):
-            quantise_w1(0, c0, H // 2)
         for t in range(PACK):
-            for g in range(RING):
+            quantise_w1(0, t * P, P)
+        for t in range(PACK):
+            for g in range(AHEAD):
                 product_pass(g, t, 0)
-        for i in range(last):
+        late = keep.tile([P, PIECE], BF16, name="late", tag="w_raw_0_1", align_bytes=DMA_ALIGN)
+        nc.scalar.activation(out=late[:], in_=looked_up(1, 3, 3 * PIECE, PIECE), func=COPY)
+        for i in range(W_LOADS):
             round_w1(1, i)
-        quantise_x(1, 0, behind="w_raw_0_%d" % last)
-        round_w1(1, last)
-        w_codes[1] = keep.tile([P, H], U32, name="w_codes_1", tag="w_raw_1_%d" % (last - 1), align_bytes=DMA_ALIGN)
+        w_codes[1] = keep.tile([P, H], U32, name="w_codes_1", align_bytes=DMA_ALIGN)
         for m0 in (0, P // 2):
             for t in range(PACK):
                 quantise_w1(1, t * P + m0, P // 2)
-        quantise_x(1, 1, behind="w_raw_1_%d" % last)
+        weave(1, 3, 4, PIECE)
+        quantise_x(1, 0, PIECE)
+        weave(1, 2, 4, 2 * PIECE)
+        quantise_x(1, PIECE, PIECE, behind="w_raw_0_2")
+        nc.vector.tensor_copy(out=woven[1][:, 3 * PIECE:S, 3], in_=late[:])
+        quantise_x(1, 2 * PIECE, PIECE, behind="w_raw_1_0")
+        quantise_x(1, 3 * PIECE, PIECE, behind="w_raw_1_3")
         for g in range(RING):
             finish_first_product(g)
 
@@ -226,14 +219,14 @@ def tile_picked_embpos_gelu_e_kernel(tc, xT, w1, w2_words, w2_scales, pos, offs,
 
         def add_pos_and_gelu(s0, n):
             g, a = divmod(s0, GROUP)
-            pre = keep.tile([P, PACK, n], F32, name="pre_%d" % s0, align_bytes=MX_ALIGN)
+            pre = keep.tile([P, PACK, n], F32, name="pre_%d" % s0, align_bytes=DMA_ALIGN)
             nc.vector.tensor_tensor(out=pre[:], in0=acc[g][:, :, a:a + n], in1=pos_raw[g][:, :, a:a + n], op=ADD)
             nc.scalar.activation(
                 out=hidden[:, s0:s0 + n, :].rearrange("p (c e) t -> p c t e", e=4),
                 in_=pre[:].rearrange("p t (c e) -> p c t e", e=4), func=GELU)
 
         def codes_of_h(name, behind):
-            return keep.tile([P, S], U32, name=name, tag=behind, align_bytes=MX_ALIGN)
+            return keep.tile([P, S], U32, name=name, tag=behind, align_bytes=DMA_ALIGN)
 
         def quantise_h(call, codes):
             s0, n = starts(H_CALLS)[call], H_CALLS[call]

@@ -28,19 +28,19 @@ BANKS = 8
 MX_ALIGN = 64
 DMA_ALIGN = 256
 
-VECTOR_ENTRIES = 256
+
+VECTOR_ENTRIES = 512
 PIECE = 256
 W_LOAD = 128
 W_LOADS = H // W_LOAD
-W_VECTOR_COLUMNS = ((128, 0, 0, 128), (0, 0, 0, 64))
 GROUP = 128
 GROUPS = S // GROUP
 RING = 4
 AHEAD = 3
+W_VECTOR_COLUMNS = ((128, 128, 128, 128), (0, 0, 0, 64))
 STEPS = (32, 96) + (GROUP,) * (GROUPS - 2) + (64, 64)
 H_CALLS = (256, 256, 256, 128, 64, 64)
 RUNS = (256, 256, 256, 128, 128)
-VECTOR_RUN = 2
 FIRST_H_CALL_AT = S - GROUP
 FIRST_H_CALL_BEHIND = 4 * GROUP
 LATER_H_CALLS_BEHIND = 5 * GROUP
@@ -59,14 +59,17 @@ def tile_picked_embpos_gelu_e_kernel(tc, xT, w1, w2_words, w2_scales, pos, offs,
         offsets = keep.tile([P, S // STRIPE], U16, name="offsets")
 
         planes = {}
-        for z in range(PASSES):
+
+        def load_plane(z, j):
             rows = xT[z * K_PASS:(z + 1) * K_PASS, :].rearrange("(p j) c -> p j c", j=PACK)
-            for j in range(PACK):
-                plane = keep.tile([P, T], F32, name="plane_%d_%d" % (z, j), align_bytes=DMA_ALIGN)
-                nc.sync.dma_start(out=plane[:], in_=rows[:, j, :])
-                planes[z, j] = plane
-                if (z, j) == (0, 0):
-                    nc.sync.dma_start(offsets[:], offs)
+            planes[z, j] = keep.tile([P, T], F32, name="plane_%d_%d" % (z, j), align_bytes=DMA_ALIGN)
+            nc.sync.dma_start(out=planes[z, j][:], in_=rows[:, j, :])
+
+        w_rows = [w1[z * K_PASS:(z + 1) * K_PASS, :].rearrange("(p j) c -> p j c", j=PACK) for z in range(PASSES)]
+        load_plane(0, 0)
+        nc.sync.dma_start(offsets[:], offs)
+        for z, j in ((0, 1), (0, 2), (0, 3), (1, 2), (1, 0), (1, 1), (1, 3)):
+            load_plane(z, j)
 
         w2_codes = keep.tile([P, N], U32, name="w2_codes", align_bytes=DMA_ALIGN)
         w2_bytes = keep.tile([P, N], U8, name="w2_bytes", align_bytes=DMA_ALIGN)
@@ -79,10 +82,9 @@ def tile_picked_embpos_gelu_e_kernel(tc, xT, w1, w2_words, w2_scales, pos, offs,
 
         w_raw = {}
         for z in range(PASSES):
-            rows = w1[z * K_PASS:(z + 1) * K_PASS, :].rearrange("(p j) c -> p j c", j=PACK)
             for i in range(W_LOADS):
                 raw = keep.tile([P, PACK, W_LOAD], F32, name="w_raw_%d_%d" % (z, i), align_bytes=DMA_ALIGN)
-                nc.sync.dma_start(out=raw[:], in_=rows[:, :, i * W_LOAD:(i + 1) * W_LOAD])
+                nc.sync.dma_start(out=raw[:], in_=w_rows[z][:, :, i * W_LOAD:(i + 1) * W_LOAD])
                 w_raw[z, i] = raw
 
         pos_rows = pos.rearrange("(p t) s -> p t s", t=PACK)
@@ -97,30 +99,18 @@ def tile_picked_embpos_gelu_e_kernel(tc, xT, w1, w2_words, w2_scales, pos, offs,
             nc.sync.dma_start(out=w2_bytes[QUADRANT * q:QUADRANT * q + SCALE_ROWS, :].bitcast(I32),
                               in_=w2_scales[0, SCALE_ROWS * q:SCALE_ROWS * (q + 1), :].bitcast(I32))
 
-        picked = []
-        woven = []
+        woven = {}
         for z in range(PASSES):
-            picked.append(keep.tile([P, PACK, S], BF16, name="picked_%d" % z, align_bytes=MX_ALIGN))
-            woven.append(keep.tile([P, S, PACK], BF16, name="woven_%d" % z, align_bytes=MX_ALIGN))
+            woven[z] = keep.tile([P, S, PACK], BF16, name="woven_%d" % z, align_bytes=MX_ALIGN)
         x_codes = {}
         x_bytes = {}
 
-        def looked_up(z, j, s0, n):
-            return planes[z, j][:].indirect(offsets[:, s0 // STRIPE:(s0 + n) // STRIPE])
-
-        def gather(z, j, order=(1, 2, 3)):
-            nc.vector.tensor_copy(out=woven[z][:, 0:VECTOR_ENTRIES, j], in_=looked_up(z, j, 0, VECTOR_ENTRIES))
-            for piece in order:
-                s0 = piece * PIECE
-                nc.scalar.activation(out=picked[z][:, j, s0:s0 + PIECE], in_=looked_up(z, j, s0, PIECE), func=COPY)
-
-        def weave(z, j0, j1, s0):
-            nc.vector.tensor_copy(out=woven[z][:, s0:s0 + PIECE, j0:j1],
-                                  in_=picked[z][:, j0:j1, s0:s0 + PIECE].rearrange("p j c -> p c j"))
-
-        def weave_planes(z, j0, j1):
-            for s0 in range(VECTOR_ENTRIES, S, PIECE):
-                weave(z, j0, j1, s0)
+        def gather(engine, z, j, s0, n):
+            picked = planes[z, j][:].indirect(offsets[:, s0 // STRIPE:(s0 + n) // STRIPE])
+            if engine == "vector":
+                nc.vector.tensor_copy(out=woven[z][:, s0:s0 + n, j], in_=picked)
+            else:
+                nc.scalar.activation(out=woven[z][:, s0:s0 + n, j], in_=picked, func=COPY)
 
         def quantise_x(z, s0, n, behind=None):
             name = "x_codes_%d_%d" % (z, s0)
@@ -132,35 +122,21 @@ def tile_picked_embpos_gelu_e_kernel(tc, xT, w1, w2_words, w2_scales, pos, offs,
                 x_codes[z, (s0 + a) // GROUP] = codes[:, a:a + GROUP]
                 x_bytes[z, (s0 + a) // GROUP] = scales[:, a:a + GROUP]
 
-        for j in range(PACK):
-            gather(0, j)
-            weave_planes(0, j, j + 1)
-        quantise_x(0, 0, HALF)
-        quantise_x(0, HALF, HALF)
-        gather(1, 0)
-        gather(1, 1)
-        weave_planes(1, 0, 2)
-        gather(1, 2, (1, 3, 2))
-        weave(1, 2, 3, PIECE)
-        weave(1, 2, 3, 3 * PIECE)
-        gather(1, 3, (1, 2))
-
         w_rounded = []
-        w_codes = {}
+        w_codes = []
         w_bytes = []
         for z in range(PASSES):
-            w_rounded.append(keep.tile([P, PACK, P, PACK], BF16, name="w_rounded_%d" % z, align_bytes=MX_ALIGN))
+            w_rounded.append(keep.tile([P, PACK, P, PACK], BF16, name="w_rounded_%d" % z, align_bytes=DMA_ALIGN))
+            w_codes.append(keep.tile([P, H], U32, name="w_codes_%d" % z, align_bytes=DMA_ALIGN))
             w_bytes.append(keep.tile([P, H], U8, name="w_bytes_%d" % z, align_bytes=MX_ALIGN))
 
-        def round_w1(z, i):
-            m_all = W_LOAD // PACK
-            m_scalar = m_all - W_VECTOR_COLUMNS[z][i] // PACK
-            dst = w_rounded[z][:].rearrange("p t m j -> p m j t")[:, i * m_all:(i + 1) * m_all]
-            src = w_raw[z, i][:].rearrange("p j (m t) -> p m j t", t=PACK)
-            if m_scalar > 0:
-                nc.scalar.activation(out=dst[:, 0:m_scalar], in_=src[:, 0:m_scalar], func=COPY)
-            if m_scalar < m_all:
-                nc.vector.tensor_copy(out=dst[:, m_scalar:m_all], in_=src[:, m_scalar:m_all])
+        def round_w1(engine, z, raw, c0, n):
+            dst = w_rounded[z][:].rearrange("p t m j -> p m j t")[:, c0 // PACK:(c0 + n) // PACK]
+            src = raw.rearrange("p j (m t) -> p m j t", t=PACK)
+            if engine == "vector":
+                nc.vector.tensor_copy(out=dst, in_=src)
+            else:
+                nc.scalar.activation(out=dst, in_=src, func=COPY)
 
         def quantise_w1(z, c0, width):
             values = w_rounded[z][:].rearrange("p t m j -> p (t m j)")
@@ -187,30 +163,39 @@ def tile_picked_embpos_gelu_e_kernel(tc, xT, w1, w2_words, w2_scales, pos, offs,
             for t, z in passes:
                 product_pass(g, t, z, stop=((t, z) == passes[-1]))
 
-        last = W_LOADS - 1
+        def round_load(z, i):
+            n = W_VECTOR_COLUMNS[z][i]
+            if n > 0:
+                round_w1("vector", z, w_raw[z, i][:, :, 0:n], i * W_LOAD, n)
+            if n < W_LOAD:
+                round_w1("scalar", z, w_raw[z, i][:, :, n:W_LOAD], i * W_LOAD + n, W_LOAD - n)
+
+        for z, j in ((0, 0), (0, 1), (0, 2), (0, 3), (1, 2), (1, 0), (1, 1)):
+            n = PIECE if (z, j) == (1, 2) else VECTOR_ENTRIES
+            gather("vector", z, j, 0, n)
+            gather("scalar", z, j, n, S - n)
+            if (z, j) == (0, 3):
+                quantise_x(0, 0, HALF)
+                quantise_x(0, HALF, HALF)
+        gather("vector", 1, 3, 0, PIECE)
+        for s0 in range(PIECE, S, PIECE):
+            gather("scalar", 1, 3, s0, PIECE)
         for i in range(W_LOADS):
-            round_w1(0, i)
-        w_codes[0] = keep.tile([P, H], U32, name="w_codes_0", align_bytes=DMA_ALIGN)
+            round_load(0, i)
         for t in range(PACK):
             quantise_w1(0, t * P, P)
         for t in range(PACK):
             for g in range(AHEAD):
                 product_pass(g, t, 0)
-        late = keep.tile([P, PIECE], BF16, name="late", tag="w_raw_0_1", align_bytes=DMA_ALIGN)
-        nc.scalar.activation(out=late[:], in_=looked_up(1, 3, 3 * PIECE, PIECE), func=COPY)
         for i in range(W_LOADS):
-            round_w1(1, i)
-        w_codes[1] = keep.tile([P, H], U32, name="w_codes_1", align_bytes=DMA_ALIGN)
+            round_load(1, i)
         for m0 in (0, P // 2):
             for t in range(PACK):
                 quantise_w1(1, t * P + m0, P // 2)
-        weave(1, 3, 4, PIECE)
         quantise_x(1, 0, PIECE)
-        weave(1, 2, 4, 2 * PIECE)
-        quantise_x(1, PIECE, PIECE, behind="w_raw_0_2")
-        nc.vector.tensor_copy(out=woven[1][:, 3 * PIECE:S, 3], in_=late[:])
+        quantise_x(1, PIECE, PIECE)
         quantise_x(1, 2 * PIECE, PIECE, behind="w_raw_1_0")
-        quantise_x(1, 3 * PIECE, PIECE, behind="w_raw_1_3")
+        quantise_x(1, 3 * PIECE, PIECE, behind="w_rounded_1")
         for g in range(RING):
             finish_first_product(g)
 
@@ -240,7 +225,7 @@ def tile_picked_embpos_gelu_e_kernel(tc, xT, w1, w2_words, w2_scales, pos, offs,
                                 rhs=codes[:, s0:s0 + n].bitcast(FP8X4), rhs_scale=h_bytes[:, s0:s0 + n],
                                 start=True, stop=True)
             result = keep.tile([P, n], F32, name="result_%d" % r, align_bytes=DMA_ALIGN)
-            if r == VECTOR_RUN:
+            if r == 2:
                 nc.vector.tensor_copy(out=result[:], in_=sums[:])
             else:
                 nc.scalar.activation(out=result[:], in_=sums[:], func=COPY)

@@ -29,7 +29,7 @@ MX_ALIGN = 64
 DMA_ALIGN = 256
 
 
-VECTOR_ENTRIES = 512
+VECTOR_ENTRIES = (512, 608)
 PIECE = 256
 W_LOAD = 128
 W_LOADS = H // W_LOAD
@@ -171,7 +171,7 @@ def tile_picked_embpos_gelu_e_kernel(tc, xT, w1, w2_words, w2_scales, pos, offs,
                 round_w1("scalar", z, w_raw[z, i][:, :, n:W_LOAD], i * W_LOAD + n, W_LOAD - n)
 
         for z, j in ((0, 0), (0, 1), (0, 2), (0, 3), (1, 2), (1, 0), (1, 1)):
-            n = PIECE if (z, j) == (1, 2) else VECTOR_ENTRIES
+            n = PIECE if (z, j) == (1, 2) else VECTOR_ENTRIES[z]
             gather("vector", z, j, 0, n)
             gather("scalar", z, j, n, S - n)
             if (z, j) == (0, 3):

from contextlib import ExitStack

import concourse.mybir as mybir

K, T, S, H, N = 1024, 2048, 1024, 512, 128
FLOPS = 2 * K * H * S + 2 * H * N * S

F32 = mybir.dt.float32
BF16 = mybir.dt.bfloat16
I32 = mybir.dt.int32
U32 = mybir.dt.uint32
U16 = mybir.dt.uint16
U8 = mybir.dt.uint8
FP8X4 = mybir.dt.float8_e4m3fn_x4
COPY = mybir.ActivationFunctionType.Copy
GELU = mybir.ActivationFunctionType.Gelu_apprx_tanh
ADD = mybir.AluOpType.add

P = 128
PACK = 4
K_PASS = P * PACK
PASSES = K // K_PASS
HALF = S // 2
STRIPE = 16
QUADRANT = 32
SCALE_ROWS = 4
BANKS = 8
MX_ALIGN = 64
DMA_ALIGN = 256


VECTOR_ENTRIES = (512, 608)
PIECE = 256
W_LOAD = 128
W_LOADS = H // W_LOAD
GROUP = 128
GROUPS = S // GROUP
RING = 4
AHEAD = 3
W_VECTOR_COLUMNS = ((128, 128, 128, 128), (0, 0, 0, 64))
STEPS = (32, 96) + (GROUP,) * (GROUPS - 2) + (64, 64)
H_CALLS = (256, 256, 256, 128, 64, 64)
RUNS = (256, 256, 256, 128, 128)
FIRST_H_CALL_AT = S - GROUP
FIRST_H_CALL_BEHIND = 4 * GROUP
LATER_H_CALLS_BEHIND = 5 * GROUP


def starts(widths):
    return [sum(widths[:i]) for i in range(len(widths))]


def tile_picked_embpos_gelu_e_kernel(tc, xT, w1, w2_words, w2_scales, pos, offs, out):
    nc = tc.nc
    with ExitStack() as ctx:
        keep = ctx.enter_context(tc.tile_pool(name="keep", bufs=1))
        psum = ctx.enter_context(tc.psum_pool(name="psum", bufs=1))

        offsets = keep.tile([P, S // STRIPE], U16, name="offsets")

        planes = {}

        def load_plane(z, j):
            rows = xT[z * K_PASS:(z + 1) * K_PASS, :].rearrange("(p j) c -> p j c", j=PACK)
            planes[z, j] = keep.tile([P, T], F32, name="plane_%d_%d" % (z, j), align_bytes=DMA_ALIGN)
            nc.sync.dma_start(out=planes[z, j][:], in_=rows[:, j, :])

        w_rows = [w1[z * K_PASS:(z + 1) * K_PASS, :].rearrange("(p j) c -> p j c", j=PACK) for z in range(PASSES)]
        load_plane(0, 0)
        nc.sync.dma_start(offsets[:], offs)
        for z, j in ((0, 1), (0, 2), (0, 3), (1, 2), (1, 0), (1, 1), (1, 3)):
            load_plane(z, j)

        w2_codes = keep.tile([P, N], U32, name="w2_codes", align_bytes=DMA_ALIGN)
        w2_bytes = keep.tile([P, N], U8, name="w2_bytes", align_bytes=DMA_ALIGN)
        nc.vector.memset(w2_bytes[:].bitcast(I32), 0)

        zero = keep.tile([P, 1], F32, name="zero")
        nc.vector.memset(zero[:], 0.0)
        unread_gelu = keep.tile([P, 1], F32, name="unread_gelu")
        nc.scalar.activation(out=unread_gelu[:], in_=zero[:], func=GELU)

        w_raw = {}
        for z in range(PASSES):
            for i in range(W_LOADS):
                raw = keep.tile([P, PACK, W_LOAD], F32, name="w_raw_%d_%d" % (z, i), align_bytes=DMA_ALIGN)
                nc.sync.dma_start(out=raw[:], in_=w_rows[z][:, :, i * W_LOAD:(i + 1) * W_LOAD])
                w_raw[z, i] = raw

        pos_rows = pos.rearrange("(p t) s -> p t s", t=PACK)
        pos_raw = []
        for g in range(GROUPS):
            raw = keep.tile([P, PACK, GROUP], F32, name="pos_%d" % g, align_bytes=DMA_ALIGN)
            nc.sync.dma_start(out=raw[:], in_=pos_rows[:, :, g * GROUP:(g + 1) * GROUP])
            pos_raw.append(raw)

        nc.sync.dma_start(out=w2_codes[:].bitcast(I32), in_=w2_words[0].rearrange("p n r -> p (n r)").bitcast(I32))
        for q in range(P // QUADRANT):
            nc.sync.dma_start(out=w2_bytes[QUADRANT * q:QUADRANT * q + SCALE_ROWS, :].bitcast(I32),
                              in_=w2_scales[0, SCALE_ROWS * q:SCALE_ROWS * (q + 1), :].bitcast(I32))

        woven = {}
        for z in range(PASSES):
            woven[z] = keep.tile([P, S, PACK], BF16, name="woven_%d" % z, align_bytes=MX_ALIGN)
        x_codes = {}
        x_bytes = {}

        def gather(engine, z, j, s0, n):
            picked = planes[z, j][:].indirect(offsets[:, s0 // STRIPE:(s0 + n) // STRIPE])
            if engine == "vector":
                nc.vector.tensor_copy(out=woven[z][:, s0:s0 + n, j], in_=picked)
            else:
                nc.scalar.activation(out=woven[z][:, s0:s0 + n, j], in_=picked, func=COPY)

        def quantise_x(z, s0, n, behind=None):
            name = "x_codes_%d_%d" % (z, s0)
            codes = keep.tile([P, n], U32, name=name, tag=behind or name, align_bytes=DMA_ALIGN)
            scales = keep.tile([P, n], U8, name="x_bytes_%d_%d" % (z, s0), align_bytes=MX_ALIGN)
            nc.vector.quantize_mx(out=codes[:].bitcast(FP8X4), scales=scales[:],
                                  in_=woven[z][:, s0:s0 + n, :].rearrange("p c j -> p (c j)"))
            for a in range(0, n, GROUP):
                x_codes[z, (s0 + a) // GROUP] = codes[:, a:a + GROUP]
                x_bytes[z, (s0 + a) // GROUP] = scales[:, a:a + GROUP]

        w_rounded = []
        w_codes = []
        w_bytes = []
        for z in range(PASSES):
            w_rounded.append(keep.tile([P, PACK, P, PACK], BF16, name="w_rounded_%d" % z, align_bytes=DMA_ALIGN))
            w_codes.append(keep.tile([P, H], U32, name="w_codes_%d" % z, align_bytes=DMA_ALIGN))
            w_bytes.append(keep.tile([P, H], U8, name="w_bytes_%d" % z, align_bytes=MX_ALIGN))

        def round_w1(engine, z, raw, c0, n):
            dst = w_rounded[z][:].rearrange("p t m j -> p m j t")[:, c0 // PACK:(c0 + n) // PACK]
            src = raw.rearrange("p j (m t) -> p m j t", t=PACK)
            if engine == "vector":
                nc.vector.tensor_copy(out=dst, in_=src)
            else:
                nc.scalar.activation(out=dst, in_=src, func=COPY)

        def quantise_w1(z, c0, width):
            values = w_rounded[z][:].rearrange("p t m j -> p (t m j)")
            nc.vector.quantize_mx(out=w_codes[z][:, c0:c0 + width].bitcast(FP8X4), scales=w_bytes[z][:, c0:c0 + width],
                                  in_=values[:, PACK * c0:PACK * (c0 + width)])

        acc = {}

        def product_pass(g, t, z, stop=False):
            start = g not in acc
            if start:
                acc[g] = psum.tile([P, PACK, GROUP], F32, name="acc_%d" % g, tag="bank_%d" % (g % RING))
            nc.tensor.matmul_mx(
                out=acc[g][:, t, :],
                lhsT=w_codes[z][:, t * P:(t + 1) * P].bitcast(FP8X4),
                lhsT_scale=w_bytes[z][:, t * P:(t + 1) * P],
                rhs=x_codes[z, g].bitcast(FP8X4),
                rhs_scale=x_bytes[z, g],
                start=start, stop=stop)

        def finish_first_product(g):
            order = list(range(PACK)) if g == 0 else list(reversed(range(PACK)))
            passes = [(t, 1) for t in order] + [(t, 0) for t in order if g >= AHEAD]
            for t, z in passes:
                product_pass(g, t, z, stop=((t, z) == passes[-1]))

        def round_load(z, i):
            n = W_VECTOR_COLUMNS[z][i]
            if n > 0:
                round_w1("vector", z, w_raw[z, i][:, :, 0:n], i * W_LOAD, n)
            if n < W_LOAD:
                round_w1("scalar", z, w_raw[z, i][:, :, n:W_LOAD], i * W_LOAD + n, W_LOAD - n)

        for z, j in ((0, 0), (0, 1), (0, 2), (0, 3), (1, 2), (1, 0), (1, 1)):
            n = PIECE if (z, j) == (1, 2) else VECTOR_ENTRIES[z]
            gather("vector", z, j, 0, n)
            gather("scalar", z, j, n, S - n)
            if (z, j) == (0, 3):
                quantise_x(0, 0, HALF)
                quantise_x(0, HALF, HALF)
        gather("vector", 1, 3, 0, PIECE)
        for s0 in range(PIECE, S, PIECE):
            gather("scalar", 1, 3, s0, PIECE)
        for i in range(W_LOADS):
            round_load(0, i)
        for t in range(PACK):
            quantise_w1(0, t * P, P)
        for t in range(PACK):
            for g in range(AHEAD):
                product_pass(g, t, 0)
        for i in range(W_LOADS):
            round_load(1, i)
        for m0 in (0, P // 2):
            for t in range(PACK):
                quantise_w1(1, t * P + m0, P // 2)
        quantise_x(1, 0, PIECE)
        quantise_x(1, PIECE, PIECE)
        quantise_x(1, 2 * PIECE, PIECE, behind="w_raw_1_0")
        quantise_x(1, 3 * PIECE, PIECE, behind="w_rounded_1")
        for g in range(RING):
            finish_first_product(g)

        hidden = keep.tile([P, S, PACK], BF16, name="hidden", align_bytes=MX_ALIGN)
        h_bytes = keep.tile([P, S], U8, name="h_bytes", align_bytes=MX_ALIGN)

        def add_pos_and_gelu(s0, n):
            g, a = divmod(s0, GROUP)
            pre = keep.tile([P, PACK, n], F32, name="pre_%d" % s0, align_bytes=DMA_ALIGN)
            nc.vector.tensor_tensor(out=pre[:], in0=acc[g][:, :, a:a + n], in1=pos_raw[g][:, :, a:a + n], op=ADD)
            nc.scalar.activation(
                out=hidden[:, s0:s0 + n, :].rearrange("p (c e) t -> p c t e", e=4),
                in_=pre[:].rearrange("p t (c e) -> p c t e", e=4), func=GELU)

        def codes_of_h(name, behind):
            return keep.tile([P, S], U32, name=name, tag=behind, align_bytes=DMA_ALIGN)

        def quantise_h(call, codes):
            s0, n = starts(H_CALLS)[call], H_CALLS[call]
            nc.vector.quantize_mx(out=codes[:, s0:s0 + n].bitcast(FP8X4), scales=h_bytes[:, s0:s0 + n],
                                  in_=hidden[:, s0:s0 + n, :].rearrange("p c t -> p (c t)"))

        def second_product(r, codes):
            s0, n = starts(RUNS)[r], RUNS[r]
            sums = psum.tile([P, n], F32, name="sums_%d" % r, tag="bank_%d" % (RING + r % (BANKS - RING)))
            nc.tensor.matmul_mx(out=sums[:], lhsT=w2_codes[:].bitcast(FP8X4), lhsT_scale=w2_bytes[:],
                                rhs=codes[:, s0:s0 + n].bitcast(FP8X4), rhs_scale=h_bytes[:, s0:s0 + n],
                                start=True, stop=True)
            result = keep.tile([P, n], F32, name="result_%d" % r, align_bytes=DMA_ALIGN)
            if r == 2:
                nc.vector.tensor_copy(out=result[:], in_=sums[:])
            else:
                nc.scalar.activation(out=result[:], in_=sums[:], func=COPY)
            queue = nc.scalar if r == len(RUNS) - 1 else nc.sync
            queue.dma_start(out=out[:, s0:s0 + n], in_=result[:])

        for s0, n in zip(starts(STEPS), STEPS):
            add_pos_and_gelu(s0, n)
            end = s0 + n
            if end % GROUP == 0 and end // GROUP - 1 + RING < GROUPS:
                finish_first_product(end // GROUP - 1 + RING)
            if end == FIRST_H_CALL_AT:
                first_h_codes = codes_of_h("h_codes_0", behind="pre_%d" % FIRST_H_CALL_BEHIND)
                quantise_h(0, first_h_codes)

        second_product(0, first_h_codes)
        later_h_codes = codes_of_h("h_codes_1", behind="pre_%d" % LATER_H_CALLS_BEHIND)
        run_ends = [s0 + n for s0, n in zip(starts(RUNS), RUNS)]
        for call in range(1, len(H_CALLS)):
            quantise_h(call, later_h_codes)
            end = starts(H_CALLS)[call] + H_CALLS[call]
            if end in run_ends:
                second_product(run_ends.index(end), later_h_codes)
